import numpy as np
import ml_dtypes


def mxq(x, axis, fmt="e4m3"):
    dtype, down = {"e4m3": (ml_dtypes.float8_e4m3fn, 7), "e5m2": (ml_dtypes.float8_e5m2, 14)}[fmt]
    v = np.moveaxis(np.asarray(x, np.float32).astype(ml_dtypes.bfloat16).astype(np.float64), axis, -1)
    blocks = v.reshape(v.shape[:-1] + (-1, 32))
    amax = np.abs(blocks).max(-1, keepdims=True)
    byte = np.maximum(np.where(amax > 0, np.frexp(amax)[1] - 1 + 127, 0) - down, 1)
    scale = np.exp2(byte - 127.0)
    codes = (blocks / scale).astype(np.float32).astype(dtype).astype(np.float64)
    return np.moveaxis((codes * scale).reshape(v.shape), -1, axis)


WIDE = False


def mx_kscale(k):
    if not WIDE:
        return np.ones(k)
    levels = np.array([10, -10, 5, -5, 0])
    if k % 512:
        return np.exp2(np.random.permutation(np.resize(levels, k // 32))).repeat(32)
    a = np.empty((k // 512, 16))
    for p in range(k // 512):
        a[p, :8] = np.random.permutation(np.resize(levels, 8))
        for g in range(8):
            far = levels[np.abs(levels - a[p, g]) >= 10]
            a[p, g + 8] = far[np.random.randint(len(far))]
    return np.exp2(a.ravel()).repeat(32)


def f64(x):
    return np.asarray(x).astype(np.float64)


def striped(idx):
    return np.tile(idx.reshape(-1, 16).T, (8, 1)).astype(np.uint16)


def unstriped(offs):
    return offs[:16].T.reshape(-1).astype(np.int64)


E2M1 = np.array([0.0, 0.5, 1.0, 1.5, 2.0, 3.0, 4.0, 6.0, -0.0, -0.5, -1.0, -1.5, -2.0, -3.0, -4.0, -6.0])


def pack_weight(w, fmt):
    k, n = w.shape
    w = f64(np.asarray(w, np.float32).astype(ml_dtypes.bfloat16)).reshape(k // 32, 32, n)
    amax = np.abs(w).max(1)
    if fmt == "e4m3":
        byte = np.frexp(amax)[1] - 1 + 127 - 7
    else:
        mant, ex = np.frexp(amax / 6.0)
        byte = np.where(mant > 0.5, ex, ex - 1) + 127
    byte = np.clip(np.where(amax > 0, byte, 1), 1, 254)
    scaled = (w * np.exp2(127.0 - byte)[:, None, :]).reshape(k, n).astype(np.float32)
    by_word = np.ascontiguousarray(scaled.reshape(k // 512, 128, 4, n).transpose(0, 1, 3, 2))
    if fmt == "e4m3":
        words = by_word.astype(ml_dtypes.float8_e4m3fn).view(np.uint8)
    else:
        c = by_word.astype(ml_dtypes.float4_e2m1fn).view(np.uint8) & 0xF
        words = (c[..., 0::2] | (c[..., 1::2] << 4)).reshape(k // 512, 128, 2 * n)
    return np.ascontiguousarray(words), np.ascontiguousarray(byte.astype(np.uint8).reshape(k // 512, 16, n))


def unpack_weight(words, scales, fmt):
    g, _, n = scales.shape
    words = np.ascontiguousarray(words).reshape(g, 128, n, -1)
    if fmt == "e4m3":
        vals = words.view(ml_dtypes.float8_e4m3fn).astype(np.float64)
    else:
        nib = np.empty((g, 128, n, 4), np.uint8)
        nib[..., 0::2] = words & 0xF
        nib[..., 1::2] = words >> 4
        vals = E2M1[nib]
    vals = vals * np.repeat(np.exp2(scales.astype(np.float64) - 127.0), 8, axis=1)[..., None]
    return vals.transpose(0, 1, 3, 2).reshape(g * 512, n)


def gelu(v):
    return 0.5 * v * (1.0 + np.tanh(np.sqrt(2.0 / np.pi) * (v + 0.044715 * v**3)))


K, H, N, T, S = 1024, 1024, 384, 4096, 1024

def setup_inputs():
    n = np.random.standard_normal
    s = mx_kscale(K)[:, None]
    u = mx_kscale(H)[:, None]
    tab_words, tab_scales = pack_weight(n((K, T)) * s, "e4m3")
    offs = striped(np.random.permutation(T)[:S])
    w1 = (n((K, H)) / np.sqrt(K) / s * u.T).astype(np.float32)
    b1 = (0.5 * n(H) * u[:, 0]).astype(np.float32)
    ws_words, ws_scales = pack_weight(n((K, N)) / np.sqrt(K) / s, "e2m1")
    w2 = (1.5 * n((H, N)) / np.sqrt(H) / u).astype(np.float32)
    return {"tab_words": tab_words, "tab_scales": tab_scales, "offs": offs,
            "w1": w1, "b1": b1, "ws_words": ws_words, "ws_scales": ws_scales, "w2": w2}

def reference(tab_words, tab_scales, offs, w1, b1, ws_words, ws_scales, w2):
    v = unpack_weight(tab_words, tab_scales, "e4m3")[:, unstriped(offs)]
    ws = unpack_weight(ws_words, ws_scales, "e2m1")
    w1q = mxq(f64(w1), 0, "e4m3")
    w2q = mxq(f64(w2), 0, "e4m3")
    h = np.maximum((w1q.T @ v) + f64(b1)[:, None], 0.0)
    hq = mxq(h, 0, "e4m3")
    y = w2q.T @ hq
    sat = ws.T @ v
    return y / (1.0 + np.abs(sat))

@@ -1,0 +1,247 @@
+from contextlib import ExitStack
+
+import concourse.mybir as mybir
+
+K, H, N, T, S = 1024, 1024, 384, 4096, 1024
+FLOPS = 2 * S * (K * H + K * N + H * N)
+
+F32 = mybir.dt.float32
+BF16 = mybir.dt.bfloat16
+I32 = mybir.dt.int32
+U32 = mybir.dt.uint32
+U16 = mybir.dt.uint16
+U8 = mybir.dt.uint8
+FP8X4 = mybir.dt.float8_e4m3fn_x4
+FP4X4 = mybir.dt.float4_e2m1fn_x4
+ACT = mybir.ActivationFunctionType
+ALU = mybir.AluOpType
+
+P = 128
+PACK = 4
+K_PASS = P * PACK
+HALF = 512
+QUART = 256
+N_TILES = N // P
+
+
+def tile_list_site_response_saturation_kernel(
+    tc, tab_words, tab_scales, offs, w1, b1, ws_words, ws_scales, w2, out
+):
+    nc = tc.nc
+    with ExitStack() as ctx:
+        keep = ctx.enter_context(tc.tile_pool(name="keep", bufs=1))
+        shared = ctx.enter_context(tc.tile_pool(name="shared", bufs=1))
+        psum = ctx.enter_context(tc.psum_pool(name="psum", bufs=8))
+
+        def tile(shape, dtype, name):
+            return keep.tile(shape, dtype, name=name, align_bytes=64)
+
+        def placed(shape, dtype, name, kib):
+            return shared.tile(shape, dtype, name=name, align_bytes=64, offset=kib * 1024)
+
+        offsets = tile([P, S // 16], U16, "offsets")
+        nc.sync.dma_start(offsets[:], offs)
+
+        tab = [placed([P, T], I32, "tab%d" % a, 16 * a) for a in range(2)]
+        for a in range(2):
+            nc.sync.dma_start(tab[a][:], tab_words[a].rearrange("p t i -> p (t i)").bitcast(I32))
+
+        warm = tile([P, 1], F32, "warm")
+        warm_out = tile([P, 1], F32, "warm_out")
+        nc.vector.memset(warm[:], 1.0)
+        nc.scalar.activation(warm_out[:], warm[:], ACT.Abs_reciprocal_sqrt)
+
+        tab_sc = placed([P, T // 4], I32, "tab_sc", 44)
+        nc.vector.memset(tab_sc[:], 0)
+        for q in range(4):
+            nc.gpsimd.dma_start(
+                tab_sc[32 * q : 32 * q + 8, :], tab_scales[:, 4 * q : 4 * q + 4, :].bitcast(I32)
+            )
+        ws_sc = tile([P, 2, N // 4], I32, "ws_sc")
+        nc.vector.memset(ws_sc[:], 0)
+        for q in range(4):
+            nc.gpsimd.dma_start(
+                ws_sc[32 * q : 32 * q + 4, :, :],
+                ws_scales[:, 4 * q : 4 * q + 4, :].rearrange("a r n -> r a n").bitcast(I32),
+            )
+        v_sc1 = tile([P, S // 4], I32, "v_sc1")
+        nc.vector.memset(v_sc1[:], 0)
+
+        ws_w = tile([P, 2, 2 * N // 4], I32, "ws_w")
+        nc.sync.dma_start(ws_w[:], ws_words.rearrange("a p n -> p a n").bitcast(I32))
+
+        bias = tile([P, 2, PACK], F32, "bias")
+        nc.sync.dma_start(bias[:], b1.rearrange("(b p t) -> p b t", b=2, t=PACK))
+
+        w1_raw = {}
+        w2_raw = {}
+
+        def load_w1(b, a, kib):
+            w1_raw[b, a] = placed([P, PACK, K_PASS], F32, "w1_raw%d%d" % (b, a), kib)
+            nc.sync.dma_start(
+                w1_raw[b, a][:],
+                w1[a * K_PASS : (a + 1) * K_PASS, b * K_PASS : (b + 1) * K_PASS].rearrange(
+                    "(p j) c -> p j c", j=PACK
+                ),
+            )
+
+        def load_w2(b, kib):
+            w2_raw[b] = placed([P, PACK, N], F32, "w2_raw%d" % b, kib)
+            nc.sync.dma_start(
+                w2_raw[b][:], w2[b * K_PASS : (b + 1) * K_PASS, :].rearrange("(p j) n -> p j n", j=PACK)
+            )
+
+        load_w1(0, 0, 34)
+
+        v_sc = tile([P, S], U8, "v_sc")
+        nc.vector.tensor_copy(v_sc[:], tab_sc[:].bitcast(U8).indirect(offsets[:]))
+        nc.gpsimd.dma_start(v_sc1[0:100, :], v_sc[4:104, :].bitcast(I32))
+        v_w = [placed([P, S], U32, "v_w%d" % a, 42 + 4 * a) for a in range(2)]
+        nc.vector.tensor_copy(v_w[0][:], tab[0][:].bitcast(U32).indirect(offsets[:]))
+        load_w1(0, 1, 0)
+        load_w1(1, 0, 8)
+        for hf in range(2):
+            nc.vector.tensor_copy(
+                v_w[1][:, hf * HALF : (hf + 1) * HALF],
+                tab[1][:].bitcast(U32).indirect(offsets[:, hf * HALF // 16 : (hf + 1) * HALF // 16]),
+            )
+
+        load_w1(1, 1, 16)
+        load_w2(0, 24)
+
+        w1_codes = tile([P, 2, 2, K_PASS], U32, "w1_codes")
+        w1_sc = tile([P, 2, 2, K_PASS], U8, "w1_sc")
+        w2_codes = tile([P, 2 * N], U32, "w2_codes")
+        w2_sc = tile([P, 2 * N], U8, "w2_sc")
+        w2_bf = tile([P, 2, N, PACK], BF16, "w2_bf")
+        h_codes = tile([P, 2, S], U32, "h_codes")
+        h_sc = tile([P, 2, S], U8, "h_sc")
+        damp = {}
+        h_bf = {}
+
+        def quant_w1(b, a):
+            if (b, a) == (0, 0):
+                grouped = placed([P, PACK, P, PACK], BF16, "w1_bf00", 30)
+            else:
+                grouped = tile([P, PACK, P, PACK], BF16, "w1_bf%d%d" % (b, a))
+            nc.vector.tensor_copy(
+                grouped[:].rearrange("p t m j -> p m j t"),
+                w1_raw[b, a][:].rearrange("p j (m t) -> p m j t", t=PACK),
+            )
+            nc.vector.quantize_mx(
+                out=w1_codes[:, b, a, :].bitcast(FP8X4),
+                scales=w1_sc[:, b, a, :],
+                in_=grouped[:].rearrange("p t m j -> p (t m j)"),
+            )
+
+        def cast_w2(b, copy):
+            copy(
+                w2_bf[:, b, :, :].rearrange("p (c i) j -> p c j i", i=4),
+                w2_raw[b][:].rearrange("p j (c i) -> p c j i", i=4),
+            )
+
+        def quant_w2():
+            flat = w2_bf[:].rearrange("p b n j -> p (b n j)")
+            for lo, hi in ((0, 512), (512, 768)):
+                nc.vector.quantize_mx(
+                    out=w2_codes[:, lo:hi].bitcast(FP8X4),
+                    scales=w2_sc[:, lo:hi],
+                    in_=flat[:, PACK * lo : PACK * hi],
+                )
+
+        def saturation(hf):
+            cols = slice(hf * HALF, (hf + 1) * HALF)
+            mags = []
+            for s in range(N_TILES):
+                acc = psum.tile([P, HALF], F32, name="acc")
+                for a in range(2):
+                    scale = v_sc[:, cols] if a == 0 else v_sc1[:].bitcast(U8)[:, cols]
+                    nc.tensor.matmul_mx(
+                        out=acc[:],
+                        lhsT=ws_w[:, a, :].bitcast(U8)[:, 2 * s * P : 2 * (s + 1) * P].bitcast(FP4X4),
+                        lhsT_scale=ws_sc[:, a, :].bitcast(U8)[:, s * P : (s + 1) * P],
+                        rhs=v_w[a][:, cols].bitcast(FP8X4),
+                        rhs_scale=scale,
+                        start=(a == 0),
+                        stop=(a == 1),
+                    )
+                mag = tile([P, HALF], F32, "mag%d%d" % (hf, s))
+                nc.scalar.activation(mag[:], acc[:], ACT.Abs)
+                mags.append(mag)
+            for s in range(N_TILES):
+                root = tile([P, HALF], F32, "root%d%d" % (hf, s))
+                nc.scalar.activation(root[:], mags[s][:], ACT.Abs_reciprocal_sqrt, bias=1.0)
+                damp[hf, s] = tile([P, HALF], F32, "damp%d%d" % (hf, s))
+                nc.scalar.activation(damp[hf, s][:], root[:], ACT.Square)
+
+        def response(b, hf):
+            cols = slice(hf * HALF, (hf + 1) * HALF)
+            h_bf[b, hf] = tile([P, PACK, HALF], BF16, "h_bf%d%d" % (b, hf))
+            for t in range(PACK):
+                acc = psum.tile([P, HALF], F32, name="acc")
+                for a in range(2):
+                    nc.tensor.matmul_mx(
+                        out=acc[:],
+                        lhsT=w1_codes[:, b, a, t * P : (t + 1) * P].bitcast(FP8X4),
+                        lhsT_scale=w1_sc[:, b, a, t * P : (t + 1) * P],
+                        rhs=v_w[a][:, cols].bitcast(FP8X4),
+                        rhs_scale=v_sc[4 * a : P, cols],
+                        start=(a == 0),
+                        stop=(a == 1),
+                    )
+                nc.scalar.activation(h_bf[b, hf][:, t, :], acc[:], ACT.Relu, bias=bias[:, b, t : t + 1])
+
+        def quant_h(b, hf):
+            grouped = tile([P, HALF, PACK], BF16, "h_gr%d%d" % (b, hf))
+            for u in range(2):
+                nc.vector.tensor_copy(
+                    grouped[:, u * QUART : (u + 1) * QUART, :].rearrange("p (c i) t -> p c t i", i=4),
+                    h_bf[b, hf][:, :, u * QUART : (u + 1) * QUART].rearrange("p t (c i) -> p c t i", i=4),
+                )
+            for u in range(2):
+                cols = slice(hf * HALF + u * QUART, hf * HALF + (u + 1) * QUART)
+                nc.vector.quantize_mx(
+                    out=h_codes[:, b, cols].bitcast(FP8X4),
+                    scales=h_sc[:, b, cols],
+                    in_=grouped[:, u * QUART : (u + 1) * QUART, :].rearrange("p n t -> p (n t)"),
+                )
+
+        def species(hf):
+            cols = slice(hf * HALF, (hf + 1) * HALF)
+            for s in range(N_TILES):
+                acc = psum.tile([P, HALF], F32, name="acc")
+                for b in range(2):
+                    w_cols = slice(b * N + s * P, b * N + (s + 1) * P)
+                    nc.tensor.matmul_mx(
+                        out=acc[:],
+                        lhsT=w2_codes[:, w_cols].bitcast(FP8X4),
+                        lhsT_scale=w2_sc[:, w_cols],
+                        rhs=h_codes[:, b, cols].bitcast(FP8X4),
+                        rhs_scale=h_sc[:, b, cols],
+                        start=(b == 0),
+                        stop=(b == 1),
+                    )
+                res = tile([P, HALF], F32, "res%d%d" % (hf, s))
+                nc.vector.tensor_tensor(res[:], acc[:], damp[hf, s][:], ALU.mult)
+                nc.sync.dma_start(out[s * P : (s + 1) * P, cols], res[:])
+
+        saturation(0)
+        quant_w1(0, 0)
+        load_w2(1, 34)
+        quant_w1(0, 1)
+        response(0, 0)
+        quant_w1(1, 0)
+        response(0, 1)
+        quant_w1(1, 1)
+        quant_h(0, 0)
+        response(1, 0)
+        quant_h(0, 1)
+        cast_w2(0, nc.scalar.copy)
+        response(1, 1)
+        quant_h(1, 0)
+        cast_w2(1, nc.vector.tensor_copy)
+        quant_w2()
+        species(0)
+        saturation(1)
+        quant_h(1, 1)
+        species(1)

@@ -39,24 +39,29 @@ def tile_list_site_response_saturation_kernel(
         def placed(shape, dtype, name, kib):
             return shared.tile(shape, dtype, name=name, align_bytes=64, offset=kib * 1024)
 
+        def load_tab(a):
+            words = placed([P, T], I32, "tab%d" % a, 16 * a)
+            nc.sync.dma_start(words[:], tab_words[a].rearrange("p t i -> p (t i)").bitcast(I32))
+            return words
+
+        tab = [load_tab(0)]
         offsets = tile([P, S // 16], U16, "offsets")
         nc.sync.dma_start(offsets[:], offs)
 
-        tab = [placed([P, T], I32, "tab%d" % a, 16 * a) for a in range(2)]
-        for a in range(2):
-            nc.sync.dma_start(tab[a][:], tab_words[a].rearrange("p t i -> p (t i)").bitcast(I32))
-
-        warm = tile([P, 1], F32, "warm")
-        warm_out = tile([P, 1], F32, "warm_out")
+        warm = placed([P, 1], F32, "warm", 16)
+        warm_out = placed([P, 1], F32, "warm_out", 50)
         nc.vector.memset(warm[:], 1.0)
         nc.scalar.activation(warm_out[:], warm[:], ACT.Abs_reciprocal_sqrt)
 
-        tab_sc = placed([P, T // 4], I32, "tab_sc", 44)
+        tab_sc = placed([P, T // 4], I32, "tab_sc", 40)
         nc.vector.memset(tab_sc[:], 0)
-        for q in range(4):
-            nc.gpsimd.dma_start(
-                tab_sc[32 * q : 32 * q + 8, :], tab_scales[:, 4 * q : 4 * q + 4, :].bitcast(I32)
-            )
+        by_row = tab_scales.rearrange("a (q r) t -> r q a t", r=4)
+        for r in range(4):
+            nc.sync.dma_start(tab_sc[r:P:16, :], by_row[r].bitcast(I32))
+        tab.append(load_tab(1))
+        ws_w = placed([P, 2, 2 * N // 4], I32, "ws_w", 50)
+        nc.sync.dma_start(ws_w[:], ws_words.rearrange("a p n -> p a n").bitcast(I32))
+
         ws_sc = tile([P, 2, N // 4], I32, "ws_sc")
         nc.vector.memset(ws_sc[:], 0)
         for q in range(4):
@@ -67,11 +72,8 @@ def tile_list_site_response_saturation_kernel(
         v_sc1 = tile([P, S // 4], I32, "v_sc1")
         nc.vector.memset(v_sc1[:], 0)
 
-        ws_w = tile([P, 2, 2 * N // 4], I32, "ws_w")
-        nc.sync.dma_start(ws_w[:], ws_words.rearrange("a p n -> p a n").bitcast(I32))
-
         bias = tile([P, 2, PACK], F32, "bias")
-        nc.sync.dma_start(bias[:], b1.rearrange("(b p t) -> p b t", b=2, t=PACK))
+        nc.gpsimd.dma_start(bias[:], b1.rearrange("(b p t) -> p b t", b=2, t=PACK))
 
         w1_raw = {}
         w2_raw = {}
@@ -91,12 +93,12 @@ def tile_list_site_response_saturation_kernel(
                 w2_raw[b][:], w2[b * K_PASS : (b + 1) * K_PASS, :].rearrange("(p j) n -> p j n", j=PACK)
             )
 
-        load_w1(0, 0, 34)
-
         v_sc = tile([P, S], U8, "v_sc")
         nc.vector.tensor_copy(v_sc[:], tab_sc[:].bitcast(U8).indirect(offsets[:]))
-        nc.gpsimd.dma_start(v_sc1[0:100, :], v_sc[4:104, :].bitcast(I32))
+        nc.scalar.dma_start(v_sc1[0:100, :], v_sc[16:116, :].bitcast(I32))
+        load_w1(0, 0, 34)
         v_w = [placed([P, S], U32, "v_w%d" % a, 42 + 4 * a) for a in range(2)]
+        v_planes = [v_sc[:], v_sc1[:].bitcast(U8)]
         nc.vector.tensor_copy(v_w[0][:], tab[0][:].bitcast(U32).indirect(offsets[:]))
         load_w1(0, 1, 0)
         load_w1(1, 0, 8)
@@ -117,6 +119,7 @@ def tile_list_site_response_saturation_kernel(
         h_codes = tile([P, 2, S], U32, "h_codes")
         h_sc = tile([P, 2, S], U8, "h_sc")
         damp = {}
+        mags = {}
         h_bf = {}
 
         def quant_w1(b, a):
@@ -151,26 +154,26 @@ def tile_list_site_response_saturation_kernel(
 
         def saturation(hf):
             cols = slice(hf * HALF, (hf + 1) * HALF)
-            mags = []
             for s in range(N_TILES):
                 acc = psum.tile([P, HALF], F32, name="acc")
                 for a in range(2):
-                    scale = v_sc[:, cols] if a == 0 else v_sc1[:].bitcast(U8)[:, cols]
                     nc.tensor.matmul_mx(
                         out=acc[:],
                         lhsT=ws_w[:, a, :].bitcast(U8)[:, 2 * s * P : 2 * (s + 1) * P].bitcast(FP4X4),
                         lhsT_scale=ws_sc[:, a, :].bitcast(U8)[:, s * P : (s + 1) * P],
                         rhs=v_w[a][:, cols].bitcast(FP8X4),
-                        rhs_scale=scale,
+                        rhs_scale=v_planes[a][:, cols],
                         start=(a == 0),
                         stop=(a == 1),
                     )
                 mag = tile([P, HALF], F32, "mag%d%d" % (hf, s))
                 nc.scalar.activation(mag[:], acc[:], ACT.Abs)
-                mags.append(mag)
+                mags[hf, s] = mag
+
+        def damping(hf):
             for s in range(N_TILES):
                 root = tile([P, HALF], F32, "root%d%d" % (hf, s))
-                nc.scalar.activation(root[:], mags[s][:], ACT.Abs_reciprocal_sqrt, bias=1.0)
+                nc.scalar.activation(root[:], mags[hf, s][:], ACT.Abs_reciprocal_sqrt, bias=1.0)
                 damp[hf, s] = tile([P, HALF], F32, "damp%d%d" % (hf, s))
                 nc.scalar.activation(damp[hf, s][:], root[:], ACT.Square)
 
@@ -185,7 +188,7 @@ def tile_list_site_response_saturation_kernel(
                         lhsT=w1_codes[:, b, a, t * P : (t + 1) * P].bitcast(FP8X4),
                         lhsT_scale=w1_sc[:, b, a, t * P : (t + 1) * P],
                         rhs=v_w[a][:, cols].bitcast(FP8X4),
-                        rhs_scale=v_sc[4 * a : P, cols],
+                        rhs_scale=v_planes[a][:, cols],
                         start=(a == 0),
                         stop=(a == 1),
                     )
@@ -226,9 +229,11 @@ def tile_list_site_response_saturation_kernel(
                 nc.sync.dma_start(out[s * P : (s + 1) * P, cols], res[:])
 
         saturation(0)
+        damping(0)
         quant_w1(0, 0)
         load_w2(1, 34)
         quant_w1(0, 1)
+        saturation(1)
         response(0, 0)
         quant_w1(1, 0)
         response(0, 1)
@@ -241,7 +246,7 @@ def tile_list_site_response_saturation_kernel(
         quant_h(1, 0)
         cast_w2(1, nc.vector.tensor_copy)
         quant_w2()
-        species(0)
-        saturation(1)
         quant_h(1, 1)
+        damping(1)
+        species(0)
         species(1)

@@ -20,8 +20,10 @@ P = 128
 PACK = 4
 K_PASS = P * PACK
 HALF = 512
-QUART = 256
 N_TILES = N // P
+TAB_AT = (0, 18)
+H_BF_AT = ((64, 60), (56, 26))
+H_GR_AT = ((18, 84), (52, 64))
 
 
 def tile_list_site_response_saturation_kernel(
@@ -37,10 +39,10 @@ def tile_list_site_response_saturation_kernel(
             return keep.tile(shape, dtype, name=name, align_bytes=64)
 
         def placed(shape, dtype, name, kib):
-            return shared.tile(shape, dtype, name=name, align_bytes=64, offset=kib * 1024)
+            return shared.tile(shape, dtype, name=name, align_bytes=64, offset=int(kib * 1024))
 
         def load_tab(a):
-            words = placed([P, T], I32, "tab%d" % a, 16 * a)
+            words = placed([P, T], I32, "tab%d" % a, TAB_AT[a])
             nc.sync.dma_start(words[:], tab_words[a].rearrange("p t i -> p (t i)").bitcast(I32))
             return words
 
@@ -48,32 +50,29 @@ def tile_list_site_response_saturation_kernel(
         offsets = tile([P, S // 16], U16, "offsets")
         nc.sync.dma_start(offsets[:], offs)
 
-        warm = placed([P, 1], F32, "warm", 16)
-        warm_out = placed([P, 1], F32, "warm_out", 50)
+        warm = placed([P, 32], F32, "warm", TAB_AT[1] - 0.0625)
+        warm_out = placed([P, 32], F32, "warm_out", 47)
         nc.vector.memset(warm[:], 1.0)
         nc.scalar.activation(warm_out[:], warm[:], ACT.Abs_reciprocal_sqrt)
 
-        tab_sc = placed([P, T // 4], I32, "tab_sc", 40)
+        tab_sc = placed([P, T // 4], I32, "tab_sc", 42)
         nc.vector.memset(tab_sc[:], 0)
         by_row = tab_scales.rearrange("a (q r) t -> r q a t", r=4)
         for r in range(4):
             nc.sync.dma_start(tab_sc[r:P:16, :], by_row[r].bitcast(I32))
         tab.append(load_tab(1))
-        ws_w = placed([P, 2, 2 * N // 4], I32, "ws_w", 50)
+        ws_w = placed([P, 2, 2 * N // 4], I32, "ws_w", TAB_AT[1] - 1.5)
         nc.sync.dma_start(ws_w[:], ws_words.rearrange("a p n -> p a n").bitcast(I32))
 
-        ws_sc = tile([P, 2, N // 4], I32, "ws_sc")
+        ws_sc = placed([P, 2, N // 4], I32, "ws_sc", 47)
         nc.vector.memset(ws_sc[:], 0)
         for q in range(4):
-            nc.gpsimd.dma_start(
+            nc.sync.dma_start(
                 ws_sc[32 * q : 32 * q + 4, :, :],
                 ws_scales[:, 4 * q : 4 * q + 4, :].rearrange("a r n -> r a n").bitcast(I32),
             )
         v_sc1 = tile([P, S // 4], I32, "v_sc1")
         nc.vector.memset(v_sc1[:], 0)
-
-        bias = tile([P, 2, PACK], F32, "bias")
-        nc.gpsimd.dma_start(bias[:], b1.rearrange("(b p t) -> p b t", b=2, t=PACK))
 
         w1_raw = {}
         w2_raw = {}
@@ -93,54 +92,64 @@ def tile_list_site_response_saturation_kernel(
                 w2_raw[b][:], w2[b * K_PASS : (b + 1) * K_PASS, :].rearrange("(p j) n -> p j n", j=PACK)
             )
 
+        def gather_words(a, hf, words):
+            nc.vector.tensor_copy(
+                words[:], tab[a][:].bitcast(U32).indirect(offsets[:, hf * HALF // 16 : (hf + 1) * HALF // 16])
+            )
+            return words
+
         v_sc = tile([P, S], U8, "v_sc")
         nc.vector.tensor_copy(v_sc[:], tab_sc[:].bitcast(U8).indirect(offsets[:]))
-        nc.scalar.dma_start(v_sc1[0:100, :], v_sc[16:116, :].bitcast(I32))
-        load_w1(0, 0, 34)
-        v_w = [placed([P, S], U32, "v_w%d" % a, 42 + 4 * a) for a in range(2)]
+        nc.sync.dma_start(v_sc1[0:112, :], v_sc[16:P, :].bitcast(I32))
+        load_w1(0, 0, 36)
+        bias = placed([P, 2, PACK], F32, "bias", 44)
+        nc.sync.dma_start(bias[:], b1.rearrange("(b p t) -> p b t", b=2, t=PACK))
         v_planes = [v_sc[:], v_sc1[:].bitcast(U8)]
-        nc.vector.tensor_copy(v_w[0][:], tab[0][:].bitcast(U32).indirect(offsets[:]))
+        v_w = {}
+        v_w[0, 0] = gather_words(0, 0, tile([P, HALF], U32, "v_w00"))
+        v_w[0, 1] = gather_words(0, 1, placed([P, HALF], U32, "v_w01", 45))
         load_w1(0, 1, 0)
         load_w1(1, 0, 8)
-        for hf in range(2):
-            nc.vector.tensor_copy(
-                v_w[1][:, hf * HALF : (hf + 1) * HALF],
-                tab[1][:].bitcast(U32).indirect(offsets[:, hf * HALF // 16 : (hf + 1) * HALF // 16]),
-            )
-
-        load_w1(1, 1, 16)
-        load_w2(0, 24)
+        v_w[1, 0] = gather_words(1, 0, tile([P, HALF], U32, "v_w10"))
+        v_w[1, 1] = gather_words(1, 1, tile([P, HALF], U32, "v_w11"))
+        load_w1(1, 1, 18)
+        load_w2(0, 26)
 
         w1_codes = tile([P, 2, 2, K_PASS], U32, "w1_codes")
         w1_sc = tile([P, 2, 2, K_PASS], U8, "w1_sc")
         w2_codes = tile([P, 2 * N], U32, "w2_codes")
         w2_sc = tile([P, 2 * N], U8, "w2_sc")
-        w2_bf = tile([P, 2, N, PACK], BF16, "w2_bf")
         h_codes = tile([P, 2, S], U32, "h_codes")
         h_sc = tile([P, 2, S], U8, "h_sc")
         damp = {}
         mags = {}
+        roots = {}
         h_bf = {}
+        h_acc = {}
+        h_gr = {}
+        w1_bf = {}
+
+        def cast_w1(b, a):
+            w1_bf[b, a] = placed([P, PACK, P, PACK], BF16, "w1_bf%d%d" % (b, a), 72 + 4 * (2 * b + a))
+            for u in range(2):
+                nc.vector.tensor_copy(
+                    w1_bf[b, a][:, 2 * u : 2 * u + 2, :, :].rearrange("p t m j -> p m j t"),
+                    w1_raw[b, a][:].rearrange("p j (m t) -> p m j t", t=PACK)[:, :, :, 2 * u : 2 * u + 2],
+                )
 
         def quant_w1(b, a):
-            if (b, a) == (0, 0):
-                grouped = placed([P, PACK, P, PACK], BF16, "w1_bf00", 30)
-            else:
-                grouped = tile([P, PACK, P, PACK], BF16, "w1_bf%d%d" % (b, a))
-            nc.vector.tensor_copy(
-                grouped[:].rearrange("p t m j -> p m j t"),
-                w1_raw[b, a][:].rearrange("p j (m t) -> p m j t", t=PACK),
-            )
-            nc.vector.quantize_mx(
-                out=w1_codes[:, b, a, :].bitcast(FP8X4),
-                scales=w1_sc[:, b, a, :],
-                in_=grouped[:].rearrange("p t m j -> p (t m j)"),
-            )
+            for u in range(2):
+                cols = slice(2 * u * P, 2 * (u + 1) * P)
+                nc.vector.quantize_mx(
+                    out=w1_codes[:, b, a, cols].bitcast(FP8X4),
+                    scales=w1_sc[:, b, a, cols],
+                    in_=w1_bf[b, a][:, 2 * u : 2 * u + 2, :, :].rearrange("p t m j -> p (t m j)"),
+                )
 
-        def cast_w2(b, copy):
+        def cast_w2(b, cols, copy):
             copy(
-                w2_bf[:, b, :, :].rearrange("p (c i) j -> p c j i", i=4),
-                w2_raw[b][:].rearrange("p j (c i) -> p c j i", i=4),
+                w2_bf[:, b, cols, :].rearrange("p (c i) j -> p c j i", i=4),
+                w2_raw[b][:, :, cols].rearrange("p j (c i) -> p c j i", i=4),
             )
 
         def quant_w2():
@@ -161,57 +170,63 @@ def tile_list_site_response_saturation_kernel(
                         out=acc[:],
                         lhsT=ws_w[:, a, :].bitcast(U8)[:, 2 * s * P : 2 * (s + 1) * P].bitcast(FP4X4),
                         lhsT_scale=ws_sc[:, a, :].bitcast(U8)[:, s * P : (s + 1) * P],
-                        rhs=v_w[a][:, cols].bitcast(FP8X4),
+                        rhs=v_w[a, hf][:].bitcast(FP8X4),
                         rhs_scale=v_planes[a][:, cols],
                         start=(a == 0),
                         stop=(a == 1),
                     )
-                mag = tile([P, HALF], F32, "mag%d%d" % (hf, s))
-                nc.scalar.activation(mag[:], acc[:], ACT.Abs)
-                mags[hf, s] = mag
+                mags[hf, s] = tile([P, HALF], F32, "mag%d%d" % (hf, s))
+                nc.scalar.activation(mags[hf, s][:], acc[:], ACT.Abs)
+
+        def damping_root(hf):
+            for s in range(N_TILES):
+                roots[hf, s] = tile([P, HALF], F32, "root%d%d" % (hf, s))
+                nc.scalar.activation(roots[hf, s][:], mags[hf, s][:], ACT.Abs_reciprocal_sqrt, bias=1.0)
 
         def damping(hf):
             for s in range(N_TILES):
-                root = tile([P, HALF], F32, "root%d%d" % (hf, s))
-                nc.scalar.activation(root[:], mags[hf, s][:], ACT.Abs_reciprocal_sqrt, bias=1.0)
                 damp[hf, s] = tile([P, HALF], F32, "damp%d%d" % (hf, s))
-                nc.scalar.activation(damp[hf, s][:], root[:], ACT.Square)
+                nc.scalar.activation(damp[hf, s][:], roots[hf, s][:], ACT.Square)
 
-        def response(b, hf):
+        def response_pass(b, hf, a):
             cols = slice(hf * HALF, (hf + 1) * HALF)
-            h_bf[b, hf] = tile([P, PACK, HALF], BF16, "h_bf%d%d" % (b, hf))
+            if a == 1:
+                h_bf[b, hf] = placed([P, PACK, HALF], BF16, "h_bf%d%d" % (b, hf), H_BF_AT[b][hf])
             for t in range(PACK):
-                acc = psum.tile([P, HALF], F32, name="acc")
-                for a in range(2):
-                    nc.tensor.matmul_mx(
-                        out=acc[:],
-                        lhsT=w1_codes[:, b, a, t * P : (t + 1) * P].bitcast(FP8X4),
-                        lhsT_scale=w1_sc[:, b, a, t * P : (t + 1) * P],
-                        rhs=v_w[a][:, cols].bitcast(FP8X4),
-                        rhs_scale=v_planes[a][:, cols],
-                        start=(a == 0),
-                        stop=(a == 1),
+                if a == 0:
+                    h_acc[b, hf, t] = psum.tile([P, HALF], F32, name="acc")
+                nc.tensor.matmul_mx(
+                    out=h_acc[b, hf, t][:],
+                    lhsT=w1_codes[:, b, a, t * P : (t + 1) * P].bitcast(FP8X4),
+                    lhsT_scale=w1_sc[:, b, a, t * P : (t + 1) * P],
+                    rhs=v_w[a, hf][:].bitcast(FP8X4),
+                    rhs_scale=v_planes[a][:, cols],
+                    start=(a == 0),
+                    stop=(a == 1),
+                )
+                if a == 1:
+                    nc.scalar.activation(
+                        h_bf[b, hf][:, t, :], h_acc[b, hf, t][:], ACT.Relu, bias=bias[:, b, t : t + 1]
                     )
-                nc.scalar.activation(h_bf[b, hf][:, t, :], acc[:], ACT.Relu, bias=bias[:, b, t : t + 1])
+
+        def group_h(b, hf):
+            h_gr[b, hf] = placed([P, HALF, PACK], BF16, "h_gr%d%d" % (b, hf), H_GR_AT[b][hf])
+            nc.vector.tensor_copy(
+                h_gr[b, hf][:].rearrange("p (c i) t -> p c t i", i=4),
+                h_bf[b, hf][:].rearrange("p t (c i) -> p c t i", i=4),
+            )
 
         def quant_h(b, hf):
-            grouped = tile([P, HALF, PACK], BF16, "h_gr%d%d" % (b, hf))
-            for u in range(2):
-                nc.vector.tensor_copy(
-                    grouped[:, u * QUART : (u + 1) * QUART, :].rearrange("p (c i) t -> p c t i", i=4),
-                    h_bf[b, hf][:, :, u * QUART : (u + 1) * QUART].rearrange("p t (c i) -> p c t i", i=4),
-                )
-            for u in range(2):
-                cols = slice(hf * HALF + u * QUART, hf * HALF + (u + 1) * QUART)
-                nc.vector.quantize_mx(
-                    out=h_codes[:, b, cols].bitcast(FP8X4),
-                    scales=h_sc[:, b, cols],
-                    in_=grouped[:, u * QUART : (u + 1) * QUART, :].rearrange("p n t -> p (n t)"),
-                )
-
-        def species(hf):
             cols = slice(hf * HALF, (hf + 1) * HALF)
-            for s in range(N_TILES):
+            nc.vector.quantize_mx(
+                out=h_codes[:, b, cols].bitcast(FP8X4),
+                scales=h_sc[:, b, cols],
+                in_=h_gr[b, hf][:].rearrange("p n t -> p (n t)"),
+            )
+
+        def species(hf, tiles):
+            cols = slice(hf * HALF, (hf + 1) * HALF)
+            for s in tiles:
                 acc = psum.tile([P, HALF], F32, name="acc")
                 for b in range(2):
                     w_cols = slice(b * N + s * P, b * N + (s + 1) * P)
@@ -225,28 +240,49 @@ def tile_list_site_response_saturation_kernel(
                         stop=(b == 1),
                     )
                 res = tile([P, HALF], F32, "res%d%d" % (hf, s))
-                nc.vector.tensor_tensor(res[:], acc[:], damp[hf, s][:], ALU.mult)
-                nc.sync.dma_start(out[s * P : (s + 1) * P, cols], res[:])
+                width = HALF // 2 if (hf, s) == (1, N_TILES - 1) else HALF
+                for lo in range(0, HALF, width):
+                    part = slice(lo, lo + width)
+                    nc.vector.tensor_tensor(res[:, part], acc[:, part], damp[hf, s][:, part], ALU.mult)
+                    nc.sync.dma_start(
+                        out[s * P : (s + 1) * P, hf * HALF + lo : hf * HALF + lo + width], res[:, part]
+                    )
 
         saturation(0)
-        damping(0)
-        quant_w1(0, 0)
-        load_w2(1, 34)
-        quant_w1(0, 1)
         saturation(1)
-        response(0, 0)
+        damping_root(0)
+        cast_w1(0, 0)
+        load_w2(1, 36)
+        quant_w1(0, 0)
+        response_pass(0, 0, 0)
+        response_pass(0, 1, 0)
+        cast_w1(0, 1)
+        quant_w1(0, 1)
+        response_pass(0, 0, 1)
+        response_pass(0, 1, 1)
+        cast_w1(1, 0)
         quant_w1(1, 0)
-        response(0, 1)
+        response_pass(1, 0, 0)
+        cast_w1(1, 1)
+        group_h(0, 0)
         quant_w1(1, 1)
+        response_pass(1, 0, 1)
+        group_h(0, 1)
         quant_h(0, 0)
-        response(1, 0)
         quant_h(0, 1)
-        cast_w2(0, nc.scalar.copy)
-        response(1, 1)
+        w2_bf = placed([P, 2, N, PACK], BF16, "w2_bf", 64)
+        cast_w2(0, slice(0, N), nc.scalar.copy)
+        response_pass(1, 1, 0)
+        response_pass(1, 1, 1)
+        group_h(1, 0)
+        cast_w2(1, slice(0, N), nc.vector.tensor_copy)
         quant_h(1, 0)
-        cast_w2(1, nc.vector.tensor_copy)
         quant_w2()
-        quant_h(1, 1)
+        group_h(1, 1)
+        damping(0)
+        damping_root(1)
         damping(1)
-        species(0)
-        species(1)
+        species(0, [0])
+        quant_h(1, 1)
+        species(0, [1, 2])
+        species(1, [0, 1, 2])

@@ -22,6 +22,7 @@ K_PASS = P * PACK
 HALF = 512
 N_TILES = N // P
 TAB_AT = (0, 18)
+ROOTS_AT = (88, 30)
 H_BF_AT = ((64, 60), (56, 26))
 H_GR_AT = ((18, 84), (52, 64))
 
@@ -179,14 +180,14 @@ def tile_list_site_response_saturation_kernel(
                 nc.scalar.activation(mags[hf, s][:], acc[:], ACT.Abs)
 
         def damping_root(hf):
+            roots[hf] = placed([P, N_TILES, HALF], F32, "roots%d" % hf, ROOTS_AT[hf])
             for s in range(N_TILES):
-                roots[hf, s] = tile([P, HALF], F32, "root%d%d" % (hf, s))
-                nc.scalar.activation(roots[hf, s][:], mags[hf, s][:], ACT.Abs_reciprocal_sqrt, bias=1.0)
+                nc.scalar.activation(roots[hf][:, s, :], mags[hf, s][:], ACT.Abs_reciprocal_sqrt, bias=1.0)
 
         def damping(hf):
             for s in range(N_TILES):
                 damp[hf, s] = tile([P, HALF], F32, "damp%d%d" % (hf, s))
-                nc.scalar.activation(damp[hf, s][:], roots[hf, s][:], ACT.Square)
+                nc.scalar.activation(damp[hf, s][:], roots[hf][:, s, :], ACT.Square)
 
         def response_pass(b, hf, a):
             cols = slice(hf * HALF, (hf + 1) * HALF)

@@ -22,9 +22,6 @@ K_PASS = P * PACK
 HALF = 512
 N_TILES = N // P
 TAB_AT = (0, 18)
-ROOTS_AT = (88, 30)
-H_BF_AT = ((64, 60), (56, 26))
-H_GR_AT = ((18, 84), (52, 64))
 
 
 def tile_list_site_response_saturation_kernel(
@@ -129,9 +126,11 @@ def tile_list_site_response_saturation_kernel(
         h_acc = {}
         h_gr = {}
         w1_bf = {}
+        w2_bf = {}
+        y_acc = {}
 
         def cast_w1(b, a):
-            w1_bf[b, a] = placed([P, PACK, P, PACK], BF16, "w1_bf%d%d" % (b, a), 72 + 4 * (2 * b + a))
+            w1_bf[b, a] = tile([P, PACK, P, PACK], BF16, "w1_bf%d%d" % (b, a))
             for u in range(2):
                 nc.vector.tensor_copy(
                     w1_bf[b, a][:, 2 * u : 2 * u + 2, :, :].rearrange("p t m j -> p m j t"),
@@ -147,18 +146,19 @@ def tile_list_site_response_saturation_kernel(
                     in_=w1_bf[b, a][:, 2 * u : 2 * u + 2, :, :].rearrange("p t m j -> p (t m j)"),
                 )
 
-        def cast_w2(b, cols, copy):
+        def cast_w2(b, copy):
+            w2_bf[b] = tile([P, N, PACK], BF16, "w2_bf%d" % b)
             copy(
-                w2_bf[:, b, cols, :].rearrange("p (c i) j -> p c j i", i=4),
-                w2_raw[b][:, :, cols].rearrange("p j (c i) -> p c j i", i=4),
+                w2_bf[b][:].rearrange("p (c i) j -> p c j i", i=4),
+                w2_raw[b][:].rearrange("p j (c i) -> p c j i", i=4),
             )
 
-        def quant_w2():
-            flat = w2_bf[:].rearrange("p b n j -> p (b n j)")
-            for lo, hi in ((0, 512), (512, 768)):
+        def quant_w2(b):
+            flat = w2_bf[b][:].rearrange("p n j -> p (n j)")
+            for lo, hi in ((0, 256), (256, N)):
                 nc.vector.quantize_mx(
-                    out=w2_codes[:, lo:hi].bitcast(FP8X4),
-                    scales=w2_sc[:, lo:hi],
+                    out=w2_codes[:, b * N + lo : b * N + hi].bitcast(FP8X4),
+                    scales=w2_sc[:, b * N + lo : b * N + hi],
                     in_=flat[:, PACK * lo : PACK * hi],
                 )
 
@@ -180,19 +180,24 @@ def tile_list_site_response_saturation_kernel(
                 nc.scalar.activation(mags[hf, s][:], acc[:], ACT.Abs)
 
         def damping_root(hf):
-            roots[hf] = placed([P, N_TILES, HALF], F32, "roots%d" % hf, ROOTS_AT[hf])
+            roots[hf] = (
+                placed([P, N_TILES, HALF], F32, "roots1", 30) if hf else tile([P, N_TILES, HALF], F32, "roots0")
+            )
             for s in range(N_TILES):
                 nc.scalar.activation(roots[hf][:, s, :], mags[hf, s][:], ACT.Abs_reciprocal_sqrt, bias=1.0)
 
         def damping(hf):
             for s in range(N_TILES):
-                damp[hf, s] = tile([P, HALF], F32, "damp%d%d" % (hf, s))
+                if hf == 0 and s < 2:
+                    damp[hf, s] = placed([P, HALF], F32, "damp%d%d" % (hf, s), 26 + 2 * s)
+                else:
+                    damp[hf, s] = tile([P, HALF], F32, "damp%d%d" % (hf, s))
                 nc.scalar.activation(damp[hf, s][:], roots[hf][:, s, :], ACT.Square)
 
         def response_pass(b, hf, a):
             cols = slice(hf * HALF, (hf + 1) * HALF)
             if a == 1:
-                h_bf[b, hf] = placed([P, PACK, HALF], BF16, "h_bf%d%d" % (b, hf), H_BF_AT[b][hf])
+                h_bf[b, hf] = tile([P, PACK, HALF], BF16, "h_bf%d%d" % (b, hf))
             for t in range(PACK):
                 if a == 0:
                     h_acc[b, hf, t] = psum.tile([P, HALF], F32, name="acc")
@@ -211,7 +216,11 @@ def tile_list_site_response_saturation_kernel(
                     )
 
         def group_h(b, hf):
-            h_gr[b, hf] = placed([P, HALF, PACK], BF16, "h_gr%d%d" % (b, hf), H_GR_AT[b][hf])
+            h_gr[b, hf] = (
+                tile([P, HALF, PACK], BF16, "h_gr%d%d" % (b, hf))
+                if b
+                else placed([P, HALF, PACK], BF16, "h_gr%d%d" % (b, hf), 18 + 4 * hf)
+            )
             nc.vector.tensor_copy(
                 h_gr[b, hf][:].rearrange("p (c i) t -> p c t i", i=4),
                 h_bf[b, hf][:].rearrange("p t (c i) -> p c t i", i=4),
@@ -225,26 +234,29 @@ def tile_list_site_response_saturation_kernel(
                 in_=h_gr[b, hf][:].rearrange("p n t -> p (n t)"),
             )
 
-        def species(hf, tiles):
+        def species_pass(hf, b):
             cols = slice(hf * HALF, (hf + 1) * HALF)
+            for s in range(N_TILES):
+                if b == 0:
+                    y_acc[hf, s] = psum.tile([P, HALF], F32, name="acc")
+                w_cols = slice(b * N + s * P, b * N + (s + 1) * P)
+                nc.tensor.matmul_mx(
+                    out=y_acc[hf, s][:],
+                    lhsT=w2_codes[:, w_cols].bitcast(FP8X4),
+                    lhsT_scale=w2_sc[:, w_cols],
+                    rhs=h_codes[:, b, cols].bitcast(FP8X4),
+                    rhs_scale=h_sc[:, b, cols],
+                    start=(b == 0),
+                    stop=(b == 1),
+                )
+
+        def finish(hf, tiles):
             for s in tiles:
-                acc = psum.tile([P, HALF], F32, name="acc")
-                for b in range(2):
-                    w_cols = slice(b * N + s * P, b * N + (s + 1) * P)
-                    nc.tensor.matmul_mx(
-                        out=acc[:],
-                        lhsT=w2_codes[:, w_cols].bitcast(FP8X4),
-                        lhsT_scale=w2_sc[:, w_cols],
-                        rhs=h_codes[:, b, cols].bitcast(FP8X4),
-                        rhs_scale=h_sc[:, b, cols],
-                        start=(b == 0),
-                        stop=(b == 1),
-                    )
                 res = tile([P, HALF], F32, "res%d%d" % (hf, s))
                 width = HALF // 2 if (hf, s) == (1, N_TILES - 1) else HALF
                 for lo in range(0, HALF, width):
                     part = slice(lo, lo + width)
-                    nc.vector.tensor_tensor(res[:, part], acc[:, part], damp[hf, s][:, part], ALU.mult)
+                    nc.vector.tensor_tensor(res[:, part], y_acc[hf, s][:, part], damp[hf, s][:, part], ALU.mult)
                     nc.sync.dma_start(
                         out[s * P : (s + 1) * P, hf * HALF + lo : hf * HALF + lo + width], res[:, part]
                     )
@@ -265,25 +277,29 @@ def tile_list_site_response_saturation_kernel(
         quant_w1(1, 0)
         response_pass(1, 0, 0)
         cast_w1(1, 1)
-        group_h(0, 0)
         quant_w1(1, 1)
+        cast_w2(0, nc.scalar.copy)
         response_pass(1, 0, 1)
-        group_h(0, 1)
-        quant_h(0, 0)
-        quant_h(0, 1)
-        w2_bf = placed([P, 2, N, PACK], BF16, "w2_bf", 64)
-        cast_w2(0, slice(0, N), nc.scalar.copy)
         response_pass(1, 1, 0)
         response_pass(1, 1, 1)
+        group_h(0, 0)
+        group_h(0, 1)
+        quant_h(0, 0)
+        quant_w2(0)
+        quant_h(0, 1)
+        species_pass(0, 0)
+        species_pass(1, 0)
+        cast_w2(1, nc.vector.tensor_copy)
         group_h(1, 0)
-        cast_w2(1, slice(0, N), nc.vector.tensor_copy)
+        quant_w2(1)
         quant_h(1, 0)
-        quant_w2()
+        species_pass(0, 1)
         group_h(1, 1)
         damping(0)
         damping_root(1)
         damping(1)
-        species(0, [0])
+        finish(0, [0])
         quant_h(1, 1)
-        species(0, [1, 2])
-        species(1, [0, 1, 2])
+        species_pass(1, 1)
+        finish(0, [1, 2])
+        finish(1, [0, 1, 2])

@@ -48,6 +48,9 @@ def tile_list_site_response_saturation_kernel(
         offsets = tile([P, S // 16], U16, "offsets")
         nc.sync.dma_start(offsets[:], offs)
 
+        ws_w = tile([P, 2, 2 * N // 4], I32, "ws_w")
+        nc.sync.dma_start(ws_w[:], ws_words.rearrange("a p n -> p a n").bitcast(I32))
+
         warm = placed([P, 32], F32, "warm", TAB_AT[1] - 0.0625)
         warm_out = placed([P, 32], F32, "warm_out", 47)
         nc.vector.memset(warm[:], 1.0)
@@ -59,13 +62,11 @@ def tile_list_site_response_saturation_kernel(
         for r in range(4):
             nc.sync.dma_start(tab_sc[r:P:16, :], by_row[r].bitcast(I32))
         tab.append(load_tab(1))
-        ws_w = placed([P, 2, 2 * N // 4], I32, "ws_w", TAB_AT[1] - 1.5)
-        nc.sync.dma_start(ws_w[:], ws_words.rearrange("a p n -> p a n").bitcast(I32))
 
         ws_sc = placed([P, 2, N // 4], I32, "ws_sc", 47)
         nc.vector.memset(ws_sc[:], 0)
         for q in range(4):
-            nc.sync.dma_start(
+            nc.scalar.dma_start(
                 ws_sc[32 * q : 32 * q + 4, :, :],
                 ws_scales[:, 4 * q : 4 * q + 4, :].rearrange("a r n -> r a n").bitcast(I32),
             )
@@ -128,6 +129,7 @@ def tile_list_site_response_saturation_kernel(
         w1_bf = {}
         w2_bf = {}
         y_acc = {}
+        sat_acc = {}
 
         def cast_w1(b, a):
             w1_bf[b, a] = tile([P, PACK, P, PACK], BF16, "w1_bf%d%d" % (b, a))
@@ -162,22 +164,23 @@ def tile_list_site_response_saturation_kernel(
                     in_=flat[:, PACK * lo : PACK * hi],
                 )
 
-        def saturation(hf):
+        def saturation_pass(hf, a):
             cols = slice(hf * HALF, (hf + 1) * HALF)
             for s in range(N_TILES):
-                acc = psum.tile([P, HALF], F32, name="acc")
-                for a in range(2):
-                    nc.tensor.matmul_mx(
-                        out=acc[:],
-                        lhsT=ws_w[:, a, :].bitcast(U8)[:, 2 * s * P : 2 * (s + 1) * P].bitcast(FP4X4),
-                        lhsT_scale=ws_sc[:, a, :].bitcast(U8)[:, s * P : (s + 1) * P],
-                        rhs=v_w[a, hf][:].bitcast(FP8X4),
-                        rhs_scale=v_planes[a][:, cols],
-                        start=(a == 0),
-                        stop=(a == 1),
-                    )
-                mags[hf, s] = tile([P, HALF], F32, "mag%d%d" % (hf, s))
-                nc.scalar.activation(mags[hf, s][:], acc[:], ACT.Abs)
+                if a == 0:
+                    sat_acc[hf, s] = psum.tile([P, HALF], F32, name="acc")
+                nc.tensor.matmul_mx(
+                    out=sat_acc[hf, s][:],
+                    lhsT=ws_w[:, a, :].bitcast(U8)[:, 2 * s * P : 2 * (s + 1) * P].bitcast(FP4X4),
+                    lhsT_scale=ws_sc[:, a, :].bitcast(U8)[:, s * P : (s + 1) * P],
+                    rhs=v_w[a, hf][:].bitcast(FP8X4),
+                    rhs_scale=v_planes[a][:, cols],
+                    start=(a == 0),
+                    stop=(a == 1),
+                )
+                if a == 1:
+                    mags[hf, s] = tile([P, HALF], F32, "mag%d%d" % (hf, s))
+                    nc.scalar.activation(mags[hf, s][:], sat_acc[hf, s][:], ACT.Abs)
 
         def damping_root(hf):
             roots[hf] = (
@@ -261,8 +264,10 @@ def tile_list_site_response_saturation_kernel(
                         out[s * P : (s + 1) * P, hf * HALF + lo : hf * HALF + lo + width], res[:, part]
                     )
 
-        saturation(0)
-        saturation(1)
+        saturation_pass(0, 0)
+        saturation_pass(1, 0)
+        saturation_pass(0, 1)
+        saturation_pass(1, 1)
         damping_root(0)
         cast_w1(0, 0)
         load_w2(1, 36)

@@ -21,7 +21,7 @@ PACK = 4
 K_PASS = P * PACK
 HALF = 512
 N_TILES = N // P
-TAB_AT = (0, 18)
+TAB_AT = (2, 18)
 
 
 def tile_list_site_response_saturation_kernel(
@@ -44,24 +44,22 @@ def tile_list_site_response_saturation_kernel(
             nc.sync.dma_start(words[:], tab_words[a].rearrange("p t i -> p (t i)").bitcast(I32))
             return words
 
-        tab = [load_tab(0)]
         offsets = tile([P, S // 16], U16, "offsets")
         nc.sync.dma_start(offsets[:], offs)
-
         ws_w = tile([P, 2, 2 * N // 4], I32, "ws_w")
         nc.sync.dma_start(ws_w[:], ws_words.rearrange("a p n -> p a n").bitcast(I32))
-
-        warm = placed([P, 32], F32, "warm", TAB_AT[1] - 0.0625)
-        warm_out = placed([P, 32], F32, "warm_out", 47)
-        nc.vector.memset(warm[:], 1.0)
-        nc.scalar.activation(warm_out[:], warm[:], ACT.Abs_reciprocal_sqrt)
 
         tab_sc = placed([P, T // 4], I32, "tab_sc", 42)
         nc.vector.memset(tab_sc[:], 0)
         by_row = tab_scales.rearrange("a (q r) t -> r q a t", r=4)
         for r in range(4):
             nc.sync.dma_start(tab_sc[r:P:16, :], by_row[r].bitcast(I32))
-        tab.append(load_tab(1))
+
+        warm = placed([P, 32], F32, "warm", TAB_AT[1] - 0.0625)
+        warm_out = placed([P, 32], F32, "warm_out", 47)
+        nc.vector.memset(warm[:], 1.0)
+        nc.scalar.activation(warm_out[:], warm[:], ACT.Abs_reciprocal_sqrt)
+        tab = [load_tab(0), load_tab(1)]
 
         ws_sc = placed([P, 2, N // 4], I32, "ws_sc", 47)
         nc.vector.memset(ws_sc[:], 0)
@@ -107,8 +105,8 @@ def tile_list_site_response_saturation_kernel(
         v_w = {}
         v_w[0, 0] = gather_words(0, 0, tile([P, HALF], U32, "v_w00"))
         v_w[0, 1] = gather_words(0, 1, placed([P, HALF], U32, "v_w01", 45))
-        load_w1(0, 1, 0)
-        load_w1(1, 0, 8)
+        load_w1(0, 1, 2)
+        load_w1(1, 0, 10)
         v_w[1, 0] = gather_words(1, 0, tile([P, HALF], U32, "v_w10"))
         v_w[1, 1] = gather_words(1, 1, tile([P, HALF], U32, "v_w11"))
         load_w1(1, 1, 18)

@@ -59,15 +59,16 @@ def tile_list_site_response_saturation_kernel(
         warm_out = placed([P, 32], F32, "warm_out", 47)
         nc.vector.memset(warm[:], 1.0)
         nc.scalar.activation(warm_out[:], warm[:], ACT.Abs_reciprocal_sqrt)
-        tab = [load_tab(0), load_tab(1)]
+        tab = [load_tab(0)]
 
         ws_sc = placed([P, 2, N // 4], I32, "ws_sc", 47)
         nc.vector.memset(ws_sc[:], 0)
         for q in range(4):
-            nc.scalar.dma_start(
+            nc.sync.dma_start(
                 ws_sc[32 * q : 32 * q + 4, :, :],
                 ws_scales[:, 4 * q : 4 * q + 4, :].rearrange("a r n -> r a n").bitcast(I32),
             )
+        tab.append(load_tab(1))
         v_sc1 = tile([P, S // 4], I32, "v_sc1")
         nc.vector.memset(v_sc1[:], 0)
 

@@ -49,6 +49,9 @@ def tile_list_site_response_saturation_kernel(
         ws_w = tile([P, 2, 2 * N // 4], I32, "ws_w")
         nc.sync.dma_start(ws_w[:], ws_words.rearrange("a p n -> p a n").bitcast(I32))
 
+        bias = tile([P, 2, 2 * PACK], F32, "bias")
+        nc.sync.dma_start(bias[:, :, 0:PACK], b1.rearrange("(b p t) -> p b t", b=2, t=PACK))
+
         tab_sc = placed([P, T // 4], I32, "tab_sc", 42)
         nc.vector.memset(tab_sc[:], 0)
         by_row = tab_scales.rearrange("a (q r) t -> r q a t", r=4)
@@ -98,10 +101,9 @@ def tile_list_site_response_saturation_kernel(
 
         v_sc = tile([P, S], U8, "v_sc")
         nc.vector.tensor_copy(v_sc[:], tab_sc[:].bitcast(U8).indirect(offsets[:]))
-        nc.sync.dma_start(v_sc1[0:112, :], v_sc[16:P, :].bitcast(I32))
+        for q in range(4):
+            nc.sync.dma_start(v_sc1[32 * q : 32 * q + 4, :], v_sc[32 * q + 16 : 32 * q + 20, :].bitcast(I32))
         load_w1(0, 0, 36)
-        bias = placed([P, 2, PACK], F32, "bias", 44)
-        nc.sync.dma_start(bias[:], b1.rearrange("(b p t) -> p b t", b=2, t=PACK))
         v_planes = [v_sc[:], v_sc1[:].bitcast(U8)]
         v_w = {}
         v_w[0, 0] = gather_words(0, 0, tile([P, HALF], U32, "v_w00"))

@@ -46,34 +46,34 @@ def tile_list_site_response_saturation_kernel(
 
         offsets = tile([P, S // 16], U16, "offsets")
         nc.sync.dma_start(offsets[:], offs)
+        tab_sc = placed([P, T // 4], I32, "tab_sc", 33)
+        nc.sync.dma_start(tab_sc[96:P, :], tab_scales.rearrange("a q t -> (a q) t").bitcast(I32))
         ws_w = tile([P, 2, 2 * N // 4], I32, "ws_w")
         nc.sync.dma_start(ws_w[:], ws_words.rearrange("a p n -> p a n").bitcast(I32))
 
-        bias = tile([P, 2, 2 * PACK], F32, "bias")
-        nc.sync.dma_start(bias[:, :, 0:PACK], b1.rearrange("(b p t) -> p b t", b=2, t=PACK))
-
-        tab_sc = placed([P, T // 4], I32, "tab_sc", 42)
-        nc.vector.memset(tab_sc[:], 0)
-        by_row = tab_scales.rearrange("a (q r) t -> r q a t", r=4)
-        for r in range(4):
-            nc.sync.dma_start(tab_sc[r:P:16, :], by_row[r].bitcast(I32))
-
-        warm = placed([P, 32], F32, "warm", TAB_AT[1] - 0.0625)
-        warm_out = placed([P, 32], F32, "warm_out", 47)
-        nc.vector.memset(warm[:], 1.0)
-        nc.scalar.activation(warm_out[:], warm[:], ACT.Abs_reciprocal_sqrt)
-        tab = [load_tab(0)]
-
-        ws_sc = placed([P, 2, N // 4], I32, "ws_sc", 47)
-        nc.vector.memset(ws_sc[:], 0)
+        zeros = placed([P, 2, N // 4], I32, "zeros", 1.5)
+        nc.vector.memset(zeros[:], 0)
+        ws_sc = tile([P, 2, N // 4], I32, "ws_sc")
+        nc.vector.tensor_copy(ws_sc[:], zeros[:])
         for q in range(4):
             nc.sync.dma_start(
                 ws_sc[32 * q : 32 * q + 4, :, :],
                 ws_scales[:, 4 * q : 4 * q + 4, :].rearrange("a r n -> r a n").bitcast(I32),
             )
-        tab.append(load_tab(1))
-        v_sc1 = tile([P, S // 4], I32, "v_sc1")
-        nc.vector.memset(v_sc1[:], 0)
+        tab = [load_tab(0)]
+
+        bias = placed([P, 2, 2 * PACK], F32, "bias", 1.5)
+        nc.sync.dma_start(bias[:, :, 0:PACK], b1.rearrange("(b p t) -> p b t", b=2, t=PACK))
+
+        warm = tile([P, 32], F32, "warm")
+        warm_out = tile([P, 32], F32, "warm_out")
+        nc.vector.memset(warm[:], 1.0)
+        nc.scalar.activation(warm_out[:], warm[:], ACT.Abs_reciprocal_sqrt)
+
+        v_sc = [tile([P, S // 4], I32, "v_sc%d" % a) for a in range(2)]
+        for a in range(2):
+            nc.vector.memset(v_sc[a][:], 0)
+        nc.vector.memset(tab_sc[0:96, :], 0)
 
         w1_raw = {}
         w2_raw = {}
@@ -99,15 +99,22 @@ def tile_list_site_response_saturation_kernel(
             )
             return words
 
-        v_sc = tile([P, S], U8, "v_sc")
-        nc.vector.tensor_copy(v_sc[:], tab_sc[:].bitcast(U8).indirect(offsets[:]))
-        for q in range(4):
-            nc.sync.dma_start(v_sc1[32 * q : 32 * q + 4, :], v_sc[32 * q + 16 : 32 * q + 20, :].bitcast(I32))
+        picked = tile([P, S], U8, "picked")
+        nc.vector.tensor_copy(picked[:], tab_sc[:].bitcast(U8).indirect(offsets[:]))
+
+        def move_rows(a):
+            for q in range(4):
+                lo = 96 + 16 * a + 4 * q
+                nc.sync.dma_start(v_sc[a][32 * q : 32 * q + 4, :], picked[lo : lo + 4, :].bitcast(I32))
+
+        move_rows(0)
+        tab.append(load_tab(1))
+        move_rows(1)
         load_w1(0, 0, 36)
-        v_planes = [v_sc[:], v_sc1[:].bitcast(U8)]
+        v_planes = [v_sc[a][:].bitcast(U8) for a in range(2)]
         v_w = {}
         v_w[0, 0] = gather_words(0, 0, tile([P, HALF], U32, "v_w00"))
-        v_w[0, 1] = gather_words(0, 1, placed([P, HALF], U32, "v_w01", 45))
+        v_w[0, 1] = gather_words(0, 1, placed([P, HALF], U32, "v_w01", 34))
         load_w1(0, 1, 2)
         load_w1(1, 0, 10)
         v_w[1, 0] = gather_words(1, 0, tile([P, HALF], U32, "v_w10"))

@@ -51,29 +51,27 @@ def tile_list_site_response_saturation_kernel(
         ws_w = tile([P, 2, 2 * N // 4], I32, "ws_w")
         nc.sync.dma_start(ws_w[:], ws_words.rearrange("a p n -> p a n").bitcast(I32))
 
-        zeros = placed([P, 2, N // 4], I32, "zeros", 1.5)
-        nc.vector.memset(zeros[:], 0)
+        bias = tile([P, 2, 2 * PACK], F32, "bias")
+        nc.sync.dma_start(bias[:, :, 0:PACK], b1.rearrange("(b p t) -> p b t", b=2, t=PACK))
+        tab = [load_tab(0)]
+
         ws_sc = tile([P, 2, N // 4], I32, "ws_sc")
-        nc.vector.tensor_copy(ws_sc[:], zeros[:])
+        nc.gpsimd.memset(ws_sc[:], 0)
         for q in range(4):
-            nc.sync.dma_start(
+            nc.gpsimd.dma_start(
                 ws_sc[32 * q : 32 * q + 4, :, :],
                 ws_scales[:, 4 * q : 4 * q + 4, :].rearrange("a r n -> r a n").bitcast(I32),
             )
-        tab = [load_tab(0)]
-
-        bias = placed([P, 2, 2 * PACK], F32, "bias", 1.5)
-        nc.sync.dma_start(bias[:, :, 0:PACK], b1.rearrange("(b p t) -> p b t", b=2, t=PACK))
 
         warm = tile([P, 32], F32, "warm")
         warm_out = tile([P, 32], F32, "warm_out")
         nc.vector.memset(warm[:], 1.0)
         nc.scalar.activation(warm_out[:], warm[:], ACT.Abs_reciprocal_sqrt)
 
+        nc.vector.memset(tab_sc[0:96, :], 0)
         v_sc = [tile([P, S // 4], I32, "v_sc%d" % a) for a in range(2)]
         for a in range(2):
             nc.vector.memset(v_sc[a][:], 0)
-        nc.vector.memset(tab_sc[0:96, :], 0)
 
         w1_raw = {}
         w2_raw = {}
@@ -118,7 +116,7 @@ def tile_list_site_response_saturation_kernel(
         load_w1(0, 1, 2)
         load_w1(1, 0, 10)
         v_w[1, 0] = gather_words(1, 0, tile([P, HALF], U32, "v_w10"))
-        v_w[1, 1] = gather_words(1, 1, tile([P, HALF], U32, "v_w11"))
+        v_w[1, 1] = gather_words(1, 1, placed([P, HALF], U32, "v_w11", 44))
         load_w1(1, 1, 18)
         load_w2(0, 26)
 
@@ -190,20 +188,17 @@ def tile_list_site_response_saturation_kernel(
                     mags[hf, s] = tile([P, HALF], F32, "mag%d%d" % (hf, s))
                     nc.scalar.activation(mags[hf, s][:], sat_acc[hf, s][:], ACT.Abs)
 
-        def damping_root(hf):
-            roots[hf] = (
-                placed([P, N_TILES, HALF], F32, "roots1", 30) if hf else tile([P, N_TILES, HALF], F32, "roots0")
-            )
-            for s in range(N_TILES):
-                nc.scalar.activation(roots[hf][:, s, :], mags[hf, s][:], ACT.Abs_reciprocal_sqrt, bias=1.0)
+        def root(hf, s, dst):
+            roots[hf, s] = dst
+            nc.scalar.activation(dst, mags[hf, s][:], ACT.Abs_reciprocal_sqrt, bias=1.0)
 
-        def damping(hf):
-            for s in range(N_TILES):
-                if hf == 0 and s < 2:
-                    damp[hf, s] = placed([P, HALF], F32, "damp%d%d" % (hf, s), 26 + 2 * s)
-                else:
-                    damp[hf, s] = tile([P, HALF], F32, "damp%d%d" % (hf, s))
-                nc.scalar.activation(damp[hf, s][:], roots[hf][:, s, :], ACT.Square)
+        def square_on_vector(s, kib):
+            damp[0, s] = placed([P, HALF], F32, "damp0%d" % s, kib)
+            nc.vector.tensor_tensor(damp[0, s][:], roots[0, s], roots[0, s], ALU.mult)
+
+        def square(hf, s):
+            damp[hf, s] = tile([P, HALF], F32, "damp%d%d" % (hf, s))
+            nc.scalar.activation(damp[hf, s][:], roots[hf, s], ACT.Square)
 
         def response_pass(b, hf, a):
             cols = slice(hf * HALF, (hf + 1) * HALF)
@@ -275,8 +270,10 @@ def tile_list_site_response_saturation_kernel(
         saturation_pass(0, 0)
         saturation_pass(1, 0)
         saturation_pass(0, 1)
+        early = tile([P, 2, HALF], F32, "roots_early")
+        root(0, 0, early[:, 0, :])
         saturation_pass(1, 1)
-        damping_root(0)
+        root(0, 1, early[:, 1, :])
         cast_w1(0, 0)
         load_w2(1, 36)
         quant_w1(0, 0)
@@ -295,6 +292,8 @@ def tile_list_site_response_saturation_kernel(
         response_pass(1, 0, 1)
         response_pass(1, 1, 0)
         response_pass(1, 1, 1)
+        square_on_vector(0, 2)
+        square_on_vector(1, 10)
         group_h(0, 0)
         group_h(0, 1)
         quant_h(0, 0)
@@ -308,9 +307,15 @@ def tile_list_site_response_saturation_kernel(
         quant_h(1, 0)
         species_pass(0, 1)
         group_h(1, 1)
-        damping(0)
-        damping_root(1)
-        damping(1)
+        late = placed([P, 4, HALF], F32, "roots_late", 44)
+        root(0, 2, late[:, 0, :])
+        root(1, 0, late[:, 1, :])
+        square(0, 2)
+        root(1, 1, late[:, 2, :])
+        square(1, 0)
+        root(1, 2, late[:, 3, :])
+        square(1, 1)
+        square(1, 2)
         finish(0, [0])
         quant_h(1, 1)
         species_pass(1, 1)

@@ -22,6 +22,8 @@ K_PASS = P * PACK
 HALF = 512
 N_TILES = N // P
 TAB_AT = (2, 18)
+H_BANKS = {(0, 0): (0, 1, 2, 3), (0, 1): (4, 5, 0, 1), (1, 0): (6, 7, 2, 3), (1, 1): (4, 5, 0, 1)}
+Y_BANKS = ((6, 7, 2), (3, 4, 5))
 
 
 def tile_list_site_response_saturation_kernel(
@@ -31,13 +33,16 @@ def tile_list_site_response_saturation_kernel(
     with ExitStack() as ctx:
         keep = ctx.enter_context(tc.tile_pool(name="keep", bufs=1))
         shared = ctx.enter_context(tc.tile_pool(name="shared", bufs=1))
-        psum = ctx.enter_context(tc.psum_pool(name="psum", bufs=8))
+        psum = ctx.enter_context(tc.psum_pool(name="psum", bufs=1))
 
         def tile(shape, dtype, name):
             return keep.tile(shape, dtype, name=name, align_bytes=64)
 
         def placed(shape, dtype, name, kib):
             return shared.tile(shape, dtype, name=name, align_bytes=64, offset=int(kib * 1024))
+
+        def bank(name, index):
+            return psum.tile([P, HALF], F32, name=name, offset=index * 4 * HALF)
 
         def load_tab(a):
             words = placed([P, T], I32, "tab%d" % a, TAB_AT[a])
@@ -100,14 +105,15 @@ def tile_list_site_response_saturation_kernel(
         picked = tile([P, S], U8, "picked")
         nc.vector.tensor_copy(picked[:], tab_sc[:].bitcast(U8).indirect(offsets[:]))
 
-        def move_rows(a):
-            for q in range(4):
+        def move_rows(a, quadrants, queue):
+            for q in quadrants:
                 lo = 96 + 16 * a + 4 * q
-                nc.sync.dma_start(v_sc[a][32 * q : 32 * q + 4, :], picked[lo : lo + 4, :].bitcast(I32))
+                queue.dma_start(v_sc[a][32 * q : 32 * q + 4, :], picked[lo : lo + 4, :].bitcast(I32))
 
-        move_rows(0)
+        move_rows(0, range(4), nc.sync)
+        move_rows(1, range(2), nc.sync)
+        move_rows(1, range(2, 4), nc.gpsimd)
         tab.append(load_tab(1))
-        move_rows(1)
         load_w1(0, 0, 36)
         v_planes = [v_sc[a][:].bitcast(U8) for a in range(2)]
         v_w = {}
@@ -174,7 +180,7 @@ def tile_list_site_response_saturation_kernel(
             cols = slice(hf * HALF, (hf + 1) * HALF)
             for s in range(N_TILES):
                 if a == 0:
-                    sat_acc[hf, s] = psum.tile([P, HALF], F32, name="acc")
+                    sat_acc[hf, s] = bank("sat%d%d" % (hf, s), N_TILES * hf + s)
                 nc.tensor.matmul_mx(
                     out=sat_acc[hf, s][:],
                     lhsT=ws_w[:, a, :].bitcast(U8)[:, 2 * s * P : 2 * (s + 1) * P].bitcast(FP4X4),
@@ -206,7 +212,7 @@ def tile_list_site_response_saturation_kernel(
                 h_bf[b, hf] = tile([P, PACK, HALF], BF16, "h_bf%d%d" % (b, hf))
             for t in range(PACK):
                 if a == 0:
-                    h_acc[b, hf, t] = psum.tile([P, HALF], F32, name="acc")
+                    h_acc[b, hf, t] = bank("h%d%d%d" % (b, hf, t), H_BANKS[b, hf][t])
                 nc.tensor.matmul_mx(
                     out=h_acc[b, hf, t][:],
                     lhsT=w1_codes[:, b, a, t * P : (t + 1) * P].bitcast(FP8X4),
@@ -244,7 +250,7 @@ def tile_list_site_response_saturation_kernel(
             cols = slice(hf * HALF, (hf + 1) * HALF)
             for s in range(N_TILES):
                 if b == 0:
-                    y_acc[hf, s] = psum.tile([P, HALF], F32, name="acc")
+                    y_acc[hf, s] = bank("y%d%d" % (hf, s), Y_BANKS[hf][s])
                 w_cols = slice(b * N + s * P, b * N + (s + 1) * P)
                 nc.tensor.matmul_mx(
                     out=y_acc[hf, s][:],

@@ -57,7 +57,6 @@ def tile_list_site_response_saturation_kernel(
         nc.sync.dma_start(ws_w[:], ws_words.rearrange("a p n -> p a n").bitcast(I32))
 
         bias = tile([P, 2, 2 * PACK], F32, "bias")
-        nc.sync.dma_start(bias[:, :, 0:PACK], b1.rearrange("(b p t) -> p b t", b=2, t=PACK))
         tab = [load_tab(0)]
 
         ws_sc = tile([P, 2, N // 4], I32, "ws_sc")
@@ -111,9 +110,9 @@ def tile_list_site_response_saturation_kernel(
                 queue.dma_start(v_sc[a][32 * q : 32 * q + 4, :], picked[lo : lo + 4, :].bitcast(I32))
 
         move_rows(0, range(4), nc.sync)
-        move_rows(1, range(2), nc.sync)
-        move_rows(1, range(2, 4), nc.gpsimd)
         tab.append(load_tab(1))
+        move_rows(1, range(4), nc.gpsimd)
+        nc.gpsimd.dma_start(bias[:, :, 0:PACK], b1.rearrange("(b p t) -> p b t", b=2, t=PACK))
         load_w1(0, 0, 36)
         v_planes = [v_sc[a][:].bitcast(U8) for a in range(2)]
         v_w = {}

@@ -49,12 +49,12 @@ def tile_list_site_response_saturation_kernel(
             nc.sync.dma_start(words[:], tab_words[a].rearrange("p t i -> p (t i)").bitcast(I32))
             return words
 
-        offsets = tile([P, S // 16], U16, "offsets")
-        nc.sync.dma_start(offsets[:], offs)
         tab_sc = placed([P, T // 4], I32, "tab_sc", 33)
         nc.sync.dma_start(tab_sc[96:P, :], tab_scales.rearrange("a q t -> (a q) t").bitcast(I32))
-        ws_w = tile([P, 2, 2 * N // 4], I32, "ws_w")
-        nc.sync.dma_start(ws_w[:], ws_words.rearrange("a p n -> p a n").bitcast(I32))
+        offsets = tile([P, S // 16], U16, "offsets")
+        nc.sync.dma_start(offsets[:], offs)
+        ws_w = [tile([P, 2 * N // 4], I32, "ws_w0")]
+        nc.sync.dma_start(ws_w[0][:], ws_words[0].bitcast(I32))
 
         bias = tile([P, 2, 2 * PACK], F32, "bias")
         tab = [load_tab(0)]
@@ -111,9 +111,11 @@ def tile_list_site_response_saturation_kernel(
 
         move_rows(0, range(4), nc.sync)
         tab.append(load_tab(1))
+        ws_w.append(placed([P, 2 * N // 4], I32, "ws_w1", 36))
+        nc.sync.dma_start(ws_w[1][:], ws_words[1].bitcast(I32))
         move_rows(1, range(4), nc.gpsimd)
         nc.gpsimd.dma_start(bias[:, :, 0:PACK], b1.rearrange("(b p t) -> p b t", b=2, t=PACK))
-        load_w1(0, 0, 36)
+        load_w1(0, 0, 36.75)
         v_planes = [v_sc[a][:].bitcast(U8) for a in range(2)]
         v_w = {}
         v_w[0, 0] = gather_words(0, 0, tile([P, HALF], U32, "v_w00"))
@@ -121,7 +123,7 @@ def tile_list_site_response_saturation_kernel(
         load_w1(0, 1, 2)
         load_w1(1, 0, 10)
         v_w[1, 0] = gather_words(1, 0, tile([P, HALF], U32, "v_w10"))
-        v_w[1, 1] = gather_words(1, 1, placed([P, HALF], U32, "v_w11", 44))
+        v_w[1, 1] = gather_words(1, 1, placed([P, HALF], U32, "v_w11", 45))
         load_w1(1, 1, 18)
         load_w2(0, 26)
 
@@ -182,7 +184,7 @@ def tile_list_site_response_saturation_kernel(
                     sat_acc[hf, s] = bank("sat%d%d" % (hf, s), N_TILES * hf + s)
                 nc.tensor.matmul_mx(
                     out=sat_acc[hf, s][:],
-                    lhsT=ws_w[:, a, :].bitcast(U8)[:, 2 * s * P : 2 * (s + 1) * P].bitcast(FP4X4),
+                    lhsT=ws_w[a][:].bitcast(U8)[:, 2 * s * P : 2 * (s + 1) * P].bitcast(FP4X4),
                     lhsT_scale=ws_sc[:, a, :].bitcast(U8)[:, s * P : (s + 1) * P],
                     rhs=v_w[a, hf][:].bitcast(FP8X4),
                     rhs_scale=v_planes[a][:, cols],
@@ -280,7 +282,7 @@ def tile_list_site_response_saturation_kernel(
         saturation_pass(1, 1)
         root(0, 1, early[:, 1, :])
         cast_w1(0, 0)
-        load_w2(1, 36)
+        load_w2(1, 37)
         quant_w1(0, 0)
         response_pass(0, 0, 0)
         response_pass(0, 1, 0)
@@ -312,7 +314,7 @@ def tile_list_site_response_saturation_kernel(
         quant_h(1, 0)
         species_pass(0, 1)
         group_h(1, 1)
-        late = placed([P, 4, HALF], F32, "roots_late", 44)
+        late = placed([P, 4, HALF], F32, "roots_late", 45)
         root(0, 2, late[:, 0, :])
         root(1, 0, late[:, 1, :])
         square(0, 2)

@@ -22,8 +22,9 @@ K_PASS = P * PACK
 HALF = 512
 N_TILES = N // P
 TAB_AT = (2, 18)
-H_BANKS = {(0, 0): (0, 1, 2, 3), (0, 1): (4, 5, 0, 1), (1, 0): (6, 7, 2, 3), (1, 1): (4, 5, 0, 1)}
-Y_BANKS = ((6, 7, 2), (3, 4, 5))
+H_BANKS = {(0, 0): (6, 7, 0, 1), (0, 1): (2, 3, 6, 7), (1, 0): (4, 5, 0, 1), (1, 1): (2, 3, 6, 7)}
+Y_BANKS = ((4, 5, 0), (1, 2, 3))
+H_SCALAR = 96
 
 
 def tile_list_site_response_saturation_kernel(
@@ -205,7 +206,10 @@ def tile_list_site_response_saturation_kernel(
 
         def square(hf, s):
             damp[hf, s] = tile([P, HALF], F32, "damp%d%d" % (hf, s))
-            nc.scalar.activation(damp[hf, s][:], roots[hf, s], ACT.Square)
+            width = HALF // 2 if (hf, s) == (1, N_TILES - 1) else HALF
+            for lo in range(0, HALF, width):
+                part = slice(lo, lo + width)
+                nc.scalar.activation(damp[hf, s][:, part], roots[hf, s][:, part], ACT.Square)
 
         def response_pass(b, hf, a):
             cols = slice(hf * HALF, (hf + 1) * HALF)
@@ -228,16 +232,20 @@ def tile_list_site_response_saturation_kernel(
                         h_bf[b, hf][:, t, :], h_acc[b, hf, t][:], ACT.Relu, bias=bias[:, b, t : t + 1]
                     )
 
-        def group_h(b, hf):
+        def group_h(b, hf, shared_cols=0):
             h_gr[b, hf] = (
                 tile([P, HALF, PACK], BF16, "h_gr%d%d" % (b, hf))
                 if b
                 else placed([P, HALF, PACK], BF16, "h_gr%d%d" % (b, hf), 18 + 4 * hf)
             )
-            nc.vector.tensor_copy(
-                h_gr[b, hf][:].rearrange("p (c i) t -> p c t i", i=4),
-                h_bf[b, hf][:].rearrange("p t (c i) -> p c t i", i=4),
-            )
+            shares = [(nc.vector.tensor_copy, slice(shared_cols, HALF))]
+            if shared_cols:
+                shares.append((nc.scalar.copy, slice(0, shared_cols)))
+            for copy, cols in shares:
+                copy(
+                    h_gr[b, hf][:, cols, :].rearrange("p (c i) t -> p c t i", i=4),
+                    h_bf[b, hf][:, :, cols].rearrange("p t (c i) -> p c t i", i=4),
+                )
 
         def quant_h(b, hf):
             cols = slice(hf * HALF, (hf + 1) * HALF)
@@ -313,7 +321,7 @@ def tile_list_site_response_saturation_kernel(
         quant_w2(1)
         quant_h(1, 0)
         species_pass(0, 1)
-        group_h(1, 1)
+        group_h(1, 1, H_SCALAR)
         late = placed([P, 4, HALF], F32, "roots_late", 45)
         root(0, 2, late[:, 0, :])
         root(1, 0, late[:, 1, :])

@@ -24,7 +24,6 @@ N_TILES = N // P
 TAB_AT = (2, 18)
 H_BANKS = {(0, 0): (6, 7, 0, 1), (0, 1): (2, 3, 6, 7), (1, 0): (4, 5, 0, 1), (1, 1): (2, 3, 6, 7)}
 Y_BANKS = ((4, 5, 0), (1, 2, 3))
-H_SCALAR = 96
 
 
 def tile_list_site_response_saturation_kernel(
@@ -232,20 +231,16 @@ def tile_list_site_response_saturation_kernel(
                         h_bf[b, hf][:, t, :], h_acc[b, hf, t][:], ACT.Relu, bias=bias[:, b, t : t + 1]
                     )
 
-        def group_h(b, hf, shared_cols=0):
+        def group_h(b, hf):
             h_gr[b, hf] = (
                 tile([P, HALF, PACK], BF16, "h_gr%d%d" % (b, hf))
                 if b
                 else placed([P, HALF, PACK], BF16, "h_gr%d%d" % (b, hf), 18 + 4 * hf)
             )
-            shares = [(nc.vector.tensor_copy, slice(shared_cols, HALF))]
-            if shared_cols:
-                shares.append((nc.scalar.copy, slice(0, shared_cols)))
-            for copy, cols in shares:
-                copy(
-                    h_gr[b, hf][:, cols, :].rearrange("p (c i) t -> p c t i", i=4),
-                    h_bf[b, hf][:, :, cols].rearrange("p t (c i) -> p c t i", i=4),
-                )
+            nc.vector.tensor_copy(
+                h_gr[b, hf][:].rearrange("p (c i) t -> p c t i", i=4),
+                h_bf[b, hf][:].rearrange("p t (c i) -> p c t i", i=4),
+            )
 
         def quant_h(b, hf):
             cols = slice(hf * HALF, (hf + 1) * HALF)
@@ -321,7 +316,7 @@ def tile_list_site_response_saturation_kernel(
         quant_w2(1)
         quant_h(1, 0)
         species_pass(0, 1)
-        group_h(1, 1, H_SCALAR)
+        group_h(1, 1)
         late = placed([P, 4, HALF], F32, "roots_late", 45)
         root(0, 2, late[:, 0, :])
         root(1, 0, late[:, 1, :])

@@ -291,6 +291,8 @@ def tile_list_site_response_saturation_kernel(
         response_pass(0, 1, 0)
         cast_w1(0, 1)
         quant_w1(0, 1)
+        damp[0, 0] = placed([P, HALF], F32, "damp00", 2)
+        nc.scalar.activation(damp[0, 0][:, HALF // 2 :], roots[0, 0][:, HALF // 2 :], ACT.Square)
         response_pass(0, 0, 1)
         response_pass(0, 1, 1)
         cast_w1(1, 0)
@@ -302,7 +304,9 @@ def tile_list_site_response_saturation_kernel(
         response_pass(1, 0, 1)
         response_pass(1, 1, 0)
         response_pass(1, 1, 1)
-        square_on_vector(0, 2)
+        nc.vector.tensor_tensor(
+            damp[0, 0][:, : HALF // 2], roots[0, 0][:, : HALF // 2], roots[0, 0][:, : HALF // 2], ALU.mult
+        )
         square_on_vector(1, 10)
         group_h(0, 0)
         group_h(0, 1)

from contextlib import ExitStack

import concourse.mybir as mybir

K, H, N, T, S = 1024, 1024, 384, 4096, 1024
FLOPS = 2 * S * (K * H + K * N + H * N)

F32 = mybir.dt.float32
BF16 = mybir.dt.bfloat16
I32 = mybir.dt.int32
U32 = mybir.dt.uint32
U16 = mybir.dt.uint16
U8 = mybir.dt.uint8
FP8X4 = mybir.dt.float8_e4m3fn_x4
FP4X4 = mybir.dt.float4_e2m1fn_x4
ACT = mybir.ActivationFunctionType
ALU = mybir.AluOpType

P = 128
PACK = 4
K_PASS = P * PACK
HALF = 512
N_TILES = N // P
TAB_AT = (2, 18)
H_BANKS = {(0, 0): (6, 7, 0, 1), (0, 1): (2, 3, 6, 7), (1, 0): (4, 5, 0, 1), (1, 1): (2, 3, 6, 7)}
Y_BANKS = ((4, 5, 0), (1, 2, 3))


def tile_list_site_response_saturation_kernel(
    tc, tab_words, tab_scales, offs, w1, b1, ws_words, ws_scales, w2, out
):
    nc = tc.nc
    with ExitStack() as ctx:
        keep = ctx.enter_context(tc.tile_pool(name="keep", bufs=1))
        shared = ctx.enter_context(tc.tile_pool(name="shared", bufs=1))
        psum = ctx.enter_context(tc.psum_pool(name="psum", bufs=1))

        def tile(shape, dtype, name):
            return keep.tile(shape, dtype, name=name, align_bytes=64)

        def placed(shape, dtype, name, kib):
            return shared.tile(shape, dtype, name=name, align_bytes=64, offset=int(kib * 1024))

        def bank(name, index):
            return psum.tile([P, HALF], F32, name=name, offset=index * 4 * HALF)

        def load_tab(a):
            words = placed([P, T], I32, "tab%d" % a, TAB_AT[a])
            nc.sync.dma_start(words[:], tab_words[a].rearrange("p t i -> p (t i)").bitcast(I32))
            return words

        tab_sc = placed([P, T // 4], I32, "tab_sc", 33)
        nc.sync.dma_start(tab_sc[96:P, :], tab_scales.rearrange("a q t -> (a q) t").bitcast(I32))
        offsets = tile([P, S // 16], U16, "offsets")
        nc.sync.dma_start(offsets[:], offs)
        ws_w = [tile([P, 2 * N // 4], I32, "ws_w0")]
        nc.sync.dma_start(ws_w[0][:], ws_words[0].bitcast(I32))

        bias = tile([P, 2, 2 * PACK], F32, "bias")
        tab = [load_tab(0)]

        ws_sc = tile([P, 2, N // 4], I32, "ws_sc")
        nc.gpsimd.memset(ws_sc[:], 0)
        for q in range(4):
            nc.gpsimd.dma_start(
                ws_sc[32 * q : 32 * q + 4, :, :],
                ws_scales[:, 4 * q : 4 * q + 4, :].rearrange("a r n -> r a n").bitcast(I32),
            )

        warm = tile([P, 32], F32, "warm")
        warm_out = tile([P, 32], F32, "warm_out")
        nc.vector.memset(warm[:], 1.0)
        nc.scalar.activation(warm_out[:], warm[:], ACT.Abs_reciprocal_sqrt)

        nc.vector.memset(tab_sc[0:96, :], 0)
        v_sc = [tile([P, S // 4], I32, "v_sc%d" % a) for a in range(2)]
        for a in range(2):
            nc.vector.memset(v_sc[a][:], 0)

        w1_raw = {}
        w2_raw = {}

        def load_w1(b, a, kib):
            w1_raw[b, a] = placed([P, PACK, K_PASS], F32, "w1_raw%d%d" % (b, a), kib)
            nc.sync.dma_start(
                w1_raw[b, a][:],
                w1[a * K_PASS : (a + 1) * K_PASS, b * K_PASS : (b + 1) * K_PASS].rearrange(
                    "(p j) c -> p j c", j=PACK
                ),
            )

        def load_w2(b, kib):
            w2_raw[b] = placed([P, PACK, N], F32, "w2_raw%d" % b, kib)
            nc.sync.dma_start(
                w2_raw[b][:], w2[b * K_PASS : (b + 1) * K_PASS, :].rearrange("(p j) n -> p j n", j=PACK)
            )

        def gather_words(a, hf, words):
            nc.vector.tensor_copy(
                words[:], tab[a][:].bitcast(U32).indirect(offsets[:, hf * HALF // 16 : (hf + 1) * HALF // 16])
            )
            return words

        picked = tile([P, S], U8, "picked")
        nc.vector.tensor_copy(picked[:], tab_sc[:].bitcast(U8).indirect(offsets[:]))

        def move_rows(a, quadrants, queue):
            for q in quadrants:
                lo = 96 + 16 * a + 4 * q
                queue.dma_start(v_sc[a][32 * q : 32 * q + 4, :], picked[lo : lo + 4, :].bitcast(I32))

        move_rows(0, range(4), nc.sync)
        tab.append(load_tab(1))
        ws_w.append(placed([P, 2 * N // 4], I32, "ws_w1", 36))
        nc.sync.dma_start(ws_w[1][:], ws_words[1].bitcast(I32))
        move_rows(1, range(4), nc.gpsimd)
        nc.gpsimd.dma_start(bias[:, :, 0:PACK], b1.rearrange("(b p t) -> p b t", b=2, t=PACK))
        load_w1(0, 0, 36.75)
        v_planes = [v_sc[a][:].bitcast(U8) for a in range(2)]
        v_w = {}
        v_w[0, 0] = gather_words(0, 0, tile([P, HALF], U32, "v_w00"))
        v_w[0, 1] = gather_words(0, 1, placed([P, HALF], U32, "v_w01", 34))
        load_w1(0, 1, 2)
        load_w1(1, 0, 10)
        v_w[1, 0] = gather_words(1, 0, tile([P, HALF], U32, "v_w10"))
        v_w[1, 1] = gather_words(1, 1, placed([P, HALF], U32, "v_w11", 45))
        load_w1(1, 1, 18)
        load_w2(0, 26)

        w1_codes = tile([P, 2, 2, K_PASS], U32, "w1_codes")
        w1_sc = tile([P, 2, 2, K_PASS], U8, "w1_sc")
        w2_codes = tile([P, 2 * N], U32, "w2_codes")
        w2_sc = tile([P, 2 * N], U8, "w2_sc")
        h_codes = tile([P, 2, S], U32, "h_codes")
        h_sc = tile([P, 2, S], U8, "h_sc")
        damp = {}
        mags = {}
        roots = {}
        h_bf = {}
        h_acc = {}
        h_gr = {}
        w1_bf = {}
        w2_bf = {}
        y_acc = {}
        sat_acc = {}

        def cast_w1(b, a):
            w1_bf[b, a] = tile([P, PACK, P, PACK], BF16, "w1_bf%d%d" % (b, a))
            for u in range(2):
                nc.vector.tensor_copy(
                    w1_bf[b, a][:, 2 * u : 2 * u + 2, :, :].rearrange("p t m j -> p m j t"),
                    w1_raw[b, a][:].rearrange("p j (m t) -> p m j t", t=PACK)[:, :, :, 2 * u : 2 * u + 2],
                )

        def quant_w1(b, a):
            for u in range(2):
                cols = slice(2 * u * P, 2 * (u + 1) * P)
                nc.vector.quantize_mx(
                    out=w1_codes[:, b, a, cols].bitcast(FP8X4),
                    scales=w1_sc[:, b, a, cols],
                    in_=w1_bf[b, a][:, 2 * u : 2 * u + 2, :, :].rearrange("p t m j -> p (t m j)"),
                )

        def cast_w2(b, copy):
            w2_bf[b] = tile([P, N, PACK], BF16, "w2_bf%d" % b)
            copy(
                w2_bf[b][:].rearrange("p (c i) j -> p c j i", i=4),
                w2_raw[b][:].rearrange("p j (c i) -> p c j i", i=4),
            )

        def quant_w2(b):
            flat = w2_bf[b][:].rearrange("p n j -> p (n j)")
            for lo, hi in ((0, 256), (256, N)):
                nc.vector.quantize_mx(
                    out=w2_codes[:, b * N + lo : b * N + hi].bitcast(FP8X4),
                    scales=w2_sc[:, b * N + lo : b * N + hi],
                    in_=flat[:, PACK * lo : PACK * hi],
                )

        def saturation_pass(hf, a):
            cols = slice(hf * HALF, (hf + 1) * HALF)
            for s in range(N_TILES):
                if a == 0:
                    sat_acc[hf, s] = bank("sat%d%d" % (hf, s), N_TILES * hf + s)
                nc.tensor.matmul_mx(
                    out=sat_acc[hf, s][:],
                    lhsT=ws_w[a][:].bitcast(U8)[:, 2 * s * P : 2 * (s + 1) * P].bitcast(FP4X4),
                    lhsT_scale=ws_sc[:, a, :].bitcast(U8)[:, s * P : (s + 1) * P],
                    rhs=v_w[a, hf][:].bitcast(FP8X4),
                    rhs_scale=v_planes[a][:, cols],
                    start=(a == 0),
                    stop=(a == 1),
                )
                if a == 1:
                    mags[hf, s] = tile([P, HALF], F32, "mag%d%d" % (hf, s))
                    nc.scalar.activation(mags[hf, s][:], sat_acc[hf, s][:], ACT.Abs)

        def root(hf, s, dst):
            roots[hf, s] = dst
            nc.scalar.activation(dst, mags[hf, s][:], ACT.Abs_reciprocal_sqrt, bias=1.0)

        def square_on_vector(s, kib):
            damp[0, s] = placed([P, HALF], F32, "damp0%d" % s, kib)
            nc.vector.tensor_tensor(damp[0, s][:], roots[0, s], roots[0, s], ALU.mult)

        def square(hf, s):
            damp[hf, s] = tile([P, HALF], F32, "damp%d%d" % (hf, s))
            width = HALF // 2 if (hf, s) == (1, N_TILES - 1) else HALF
            for lo in range(0, HALF, width):
                part = slice(lo, lo + width)
                nc.scalar.activation(damp[hf, s][:, part], roots[hf, s][:, part], ACT.Square)

        def response_pass(b, hf, a):
            cols = slice(hf * HALF, (hf + 1) * HALF)
            if a == 1:
                h_bf[b, hf] = tile([P, PACK, HALF], BF16, "h_bf%d%d" % (b, hf))
            for t in range(PACK):
                if a == 0:
                    h_acc[b, hf, t] = bank("h%d%d%d" % (b, hf, t), H_BANKS[b, hf][t])
                nc.tensor.matmul_mx(
                    out=h_acc[b, hf, t][:],
                    lhsT=w1_codes[:, b, a, t * P : (t + 1) * P].bitcast(FP8X4),
                    lhsT_scale=w1_sc[:, b, a, t * P : (t + 1) * P],
                    rhs=v_w[a, hf][:].bitcast(FP8X4),
                    rhs_scale=v_planes[a][:, cols],
                    start=(a == 0),
                    stop=(a == 1),
                )
                if a == 1:
                    nc.scalar.activation(
                        h_bf[b, hf][:, t, :], h_acc[b, hf, t][:], ACT.Relu, bias=bias[:, b, t : t + 1]
                    )

        def group_h(b, hf):
            h_gr[b, hf] = (
                tile([P, HALF, PACK], BF16, "h_gr%d%d" % (b, hf))
                if b
                else placed([P, HALF, PACK], BF16, "h_gr%d%d" % (b, hf), 18 + 4 * hf)
            )
            nc.vector.tensor_copy(
                h_gr[b, hf][:].rearrange("p (c i) t -> p c t i", i=4),
                h_bf[b, hf][:].rearrange("p t (c i) -> p c t i", i=4),
            )

        def quant_h(b, hf):
            cols = slice(hf * HALF, (hf + 1) * HALF)
            nc.vector.quantize_mx(
                out=h_codes[:, b, cols].bitcast(FP8X4),
                scales=h_sc[:, b, cols],
                in_=h_gr[b, hf][:].rearrange("p n t -> p (n t)"),
            )

        def species_pass(hf, b):
            cols = slice(hf * HALF, (hf + 1) * HALF)
            for s in range(N_TILES):
                if b == 0:
                    y_acc[hf, s] = bank("y%d%d" % (hf, s), Y_BANKS[hf][s])
                w_cols = slice(b * N + s * P, b * N + (s + 1) * P)
                nc.tensor.matmul_mx(
                    out=y_acc[hf, s][:],
                    lhsT=w2_codes[:, w_cols].bitcast(FP8X4),
                    lhsT_scale=w2_sc[:, w_cols],
                    rhs=h_codes[:, b, cols].bitcast(FP8X4),
                    rhs_scale=h_sc[:, b, cols],
                    start=(b == 0),
                    stop=(b == 1),
                )

        def finish(hf, tiles):
            for s in tiles:
                res = tile([P, HALF], F32, "res%d%d" % (hf, s))
                width = HALF // 2 if (hf, s) == (1, N_TILES - 1) else HALF
                for lo in range(0, HALF, width):
                    part = slice(lo, lo + width)
                    nc.vector.tensor_tensor(res[:, part], y_acc[hf, s][:, part], damp[hf, s][:, part], ALU.mult)
                    nc.sync.dma_start(
                        out[s * P : (s + 1) * P, hf * HALF + lo : hf * HALF + lo + width], res[:, part]
                    )

        saturation_pass(0, 0)
        saturation_pass(1, 0)
        saturation_pass(0, 1)
        early = tile([P, 2, HALF], F32, "roots_early")
        root(0, 0, early[:, 0, :])
        saturation_pass(1, 1)
        root(0, 1, early[:, 1, :])
        cast_w1(0, 0)
        load_w2(1, 37)
        quant_w1(0, 0)
        response_pass(0, 0, 0)
        response_pass(0, 1, 0)
        cast_w1(0, 1)
        quant_w1(0, 1)
        damp[0, 0] = placed([P, HALF], F32, "damp00", 2)
        nc.scalar.activation(damp[0, 0][:, HALF // 2 :], roots[0, 0][:, HALF // 2 :], ACT.Square)
        response_pass(0, 0, 1)
        response_pass(0, 1, 1)
        cast_w1(1, 0)
        quant_w1(1, 0)
        response_pass(1, 0, 0)
        cast_w1(1, 1)
        quant_w1(1, 1)
        cast_w2(0, nc.scalar.copy)
        response_pass(1, 0, 1)
        response_pass(1, 1, 0)
        response_pass(1, 1, 1)
        nc.vector.tensor_tensor(
            damp[0, 0][:, : HALF // 2], roots[0, 0][:, : HALF // 2], roots[0, 0][:, : HALF // 2], ALU.mult
        )
        square_on_vector(1, 10)
        group_h(0, 0)
        group_h(0, 1)
        quant_h(0, 0)
        quant_w2(0)
        quant_h(0, 1)
        species_pass(0, 0)
        species_pass(1, 0)
        cast_w2(1, nc.vector.tensor_copy)
        group_h(1, 0)
        quant_w2(1)
        quant_h(1, 0)
        species_pass(0, 1)
        group_h(1, 1)
        late = placed([P, 4, HALF], F32, "roots_late", 45)
        root(0, 2, late[:, 0, :])
        root(1, 0, late[:, 1, :])
        square(0, 2)
        root(1, 1, late[:, 2, :])
        square(1, 0)
        root(1, 2, late[:, 3, :])
        square(1, 1)
        square(1, 2)
        finish(0, [0])
        quant_h(1, 1)
        species_pass(1, 1)
        finish(0, [1, 2])
        finish(1, [0, 1, 2])
